import numpy as np, ml_dtypes
CORES = [113,118,241,246]
N = 4
BF = ml_dtypes.bfloat16
def gentries(a):
    return np.ascontiguousarray(a.reshape(8, 16, -1).transpose(0, 2, 1)).reshape(8, -1)
def gtable(e):
    e = np.asarray(e); return np.ascontiguousarray(e.reshape(8, -1, 16).transpose(0, 2, 1)).reshape(128, -1).astype(np.int32)
V, B, H, C, A, RO = 768, 32, 24, 64, 3, 3
def names(rng, hub, *shape):
    g = np.arange(8).reshape((1, 8) + (1,) * (len(shape) - 2))
    return np.where(rng.random(shape) < 0.15, hub[g, rng.integers(0, 8, shape)], rng.integers(0, N * V, shape))
def place(rng, d, nm):
    return np.where(np.argsort(rng.random((N, 8, 16, V)), axis=2) < d[:, :, None, :], nm, N * V)
def plain(rng):
    hub = rng.integers(0, N * V, (8, 8))
    few = rng.choice(np.array([0.5, 1.0, 2.0, 3.0]), (N, 8, 1)) * H
    d = np.where(rng.random((N, 8, V)) < 0.03, 0, rng.integers(1, 13, (N, 8, V)))
    d = np.where(rng.random((N, 8, V)) * V < few, rng.integers(13, 17, (N, 8, V)), d)
    tall = rng.random((N, 8, 1, V)) * V < 0.5 * H
    x = (40000 * (0.7 + 0.3 * rng.random((N, 8, 1, V))) * rng.random((N, 8, 16, V))).astype(np.int64)
    x = np.where(tall, rng.integers(40000, 65536, (N, 8, 16, V)), x)
    a = rng.integers(0, V, (N, 8, RO * B)); b = names(rng, hub, N, 8, RO * B)
    return x, d, names(rng, hub, N, 8, 16, V), a, b, rng.integers(-2000, 2001, (N, 128, RO))
def pack(x, L, a, b, u):
    return {"x0": np.ascontiguousarray(x.reshape(N, 128, V)).astype(np.int32), "l0": np.ascontiguousarray(L.reshape(N, 128, V)).astype(np.int32),
            "ea": np.stack([gtable(k) for k in a]), "eb": np.stack([gtable(k) for k in b]), "u": np.ascontiguousarray(u).astype(np.int32)}
def tops(x, L):
    tab = np.concatenate([x[q] for q in range(N)] + [np.zeros((8, 16, 1), np.int64)], axis=2)
    m = np.zeros_like(x)
    for q in range(N):
        for i in range(16): m[q] = np.maximum(m[q], np.take_along_axis(tab, L[q, :, i][:, None, :], 2))
    return m, tab
def setup_inputs(rng):
    x, d, nm, a, b, u = plain(rng)
    return pack(x, place(rng, d, nm), a, b, u)
def setup_inputs_room(rng):
    x, d, nm, a, b, u = plain(rng); L = place(rng, np.minimum(d, 12), nm)
    x[:, 7, :, ::2] |= 2 ** 15; x[:, 7, :, 1::2] >>= 3; a[:, 7, :B] -= a[:, 7, :B] % 2
    for g in range(8): x[:, g, rng.permutation(16)[:5]] = 0
    for q in range(N):
        b[q, :, :B] = q * V + rng.integers(0, V, (8, B))
        e = (q + 1) % N; b[q, 7, :B] = e * V + 1 + 2 * rng.permutation(V // 2)[:B]
        for g in range(8):
            m = H + (0, 1, H)[int(rng.integers(0, 3))]
            if g == 1: m = H
            vs = np.sort(rng.permutation(V)[:m])
            if g == 1: vs[H - 1] = V - 1
            n = rng.choice(np.array([0, 1, C - 1, C, C + 1]), N)
            if g == 0: n[:] = C
            if g == 7: n[e] = max(C - B, 0)
            n[q] = 0; n[q] = 16 * H - int(np.sum(n))
            own = rng.permutation(np.repeat(np.arange(N), n))
            L[q, g][:, vs[:H]] = (own * V + rng.integers(0, V, 16 * H)).reshape(H, 16).T
            L[q, g][:, vs[H:]] = rng.integers(0, N * V, (16, m - H))
    return pack(x, L, a, b, u)
def setup_inputs_ties(rng):
    x, d, nm, a, b, u = plain(rng); h = V // 2
    base = rng.integers(0, 50000, (8, 16)); base[rng.integers(0, 8)] = rng.integers(61500, 65001, 16)
    base = np.broadcast_to(base[None, :, :, None], (N, 8, 16, h))
    x[..., :h] = np.take_along_axis(base, np.argsort(rng.random((N, 8, 16, h)), axis=2), 2)
    x[:, :, 0, :h] += rng.integers(0, 2, (N, 8, h))
    nm = (nm // V) * V + nm % h; low = d[..., :h]
    d[..., :h] = np.where(low > 12, 13, np.where(rng.random((N, 8, h)) < 0.5, 12, low)); d[..., h:] = rng.integers(1, 13, (N, 8, h))
    L = place(rng, d, nm); top = tops(x, L)[0][..., h:]
    share = rng.choice(np.array([1.0, 2.0, 6.0]), (N, 8, 1, 1)) * H
    rows = np.where(rng.random((N, 8, 1, h)) * V < share, rng.integers(12, 14, (N, 8, 1, h)), 11)
    x[..., h:] = np.where(np.argsort(rng.random((N, 8, 16, h)), axis=2) < rows, top + 1, top)
    m = rng.random(a.shape) < 0.5
    a = np.where(m, a % h, a); b = np.where(m, (b // V) * V + b % h, b)
    own = a + (np.arange(N) * V)[:, None, None]; z = N // 2 * 2
    b = np.where(rng.random(a.shape) < 0.1, own, b)
    b[0:z:2, :, ::8] = own[1:z:2, :, ::8]; b[1:z:2, :, ::8] = own[0:z:2, :, ::8]
    return pack(x, L, a, b, rng.integers(-1, 2, u.shape))
def setup_inputs_crowd(rng):
    x, d, nm, a, b, u = plain(rng); q = np.arange(N) * V
    ends = np.concatenate([q, q + V - 1, q + V // 2])
    nm = np.where(rng.random(nm.shape) < 0.5, rng.choice(ends, nm.shape), nm); b = np.where(rng.random(b.shape) < 0.5, rng.choice(ends, b.shape), b)
    nm = np.where(rng.random((N, 8, 1, V)) < 0.2, nm[:, :, :1], nm)
    nm = np.where(rng.random(nm.shape) < 0.05, q[:, None, None, None] + np.arange(V), nm)
    d = rng.choice(np.array([16, 15, 14, 13, 12, 10, 4]), (N, 8, V))
    d = np.where(np.arange(V) < rng.integers(0, V // 2, (N, 8, 1)), np.minimum(d, 12), d)
    d[:, :, 0] = np.array([16, 15, 14, 13, 12, 11, 14, 15]); d[:, :, V - 1] = np.array([13, 14, 16, 15, 11, 12, 16, 13]); d[:, :, V // 2] = rng.integers(11, 17, (N, 8))
    L = place(rng, d, nm)
    for g in (6, 7):
        o = int(rng.integers(0, N)); v = int(rng.integers(C // 16, V))
        b[:, g, :B] = o * V + v; L[:, g, :, :C // 16] = o * V + v
        x[o, g, :, v] = 0; L[o, g, rng.permutation(16)[:8], v] = N * V
    return pack(x, L, a, b, u)
def setup_inputs_quiet(rng):
    x, d, nm, a, b, u = plain(rng); g = rng.permutation(8); q = rng.permutation(N)
    d[q[0], g[2:]] = 16; d[q[1], g[2:]] = np.minimum(d[q[1], g[2:]], 12)
    d[:, g[0]] = 0; d[:, g[1]] = np.minimum(d[:, g[1]], 12); x[:, g[1], rng.permutation(16)[:5]] = 0
    d[q[2], g[1], V - 1] = 16
    z = rng.random(u.shape)
    u = np.where(z < 0.125, rng.choice(np.array([-65535, 65535]), u.shape), np.where(z < 0.375, rng.integers(-65535, 65536, u.shape), u))
    k = int(g[0]); x[:, k] = np.array(x[0, k, :, :1]); u[:, 16 * k:16 * k + 16] = np.array(u[0, 16 * k:16 * k + 16])
    return pack(x, place(rng, d, nm), a, b, u)
def setup_inputs_spread(rng):
    x, d, nm, a, b, u = plain(rng)
    x = np.minimum((np.exp2(16 * rng.random((N, 8, 1, V))) * rng.random((N, 8, 16, V))).astype(np.int64), 65535)
    d = (17 * rng.random((N, 8, V)) * rng.random((N, 8, V))).astype(np.int64)
    nm = (N * V * rng.random(nm.shape) * rng.random(nm.shape)).astype(np.int64)
    a = (V * rng.random(a.shape) * rng.random(a.shape)).astype(np.int64); b = (N * V * rng.random(b.shape) * rng.random(b.shape)).astype(np.int64)
    u = np.exp2(14 * rng.random(u.shape)).astype(np.int64) * rng.choice(np.array([-1, 1]), u.shape)
    return pack(x, place(rng, d, nm), a, b, u)
def check_inputs(d):
    bad = []
    for k, lo, hi in (("x0", 0, 65535), ("l0", 0, N * V), ("ea", 0, V - 1), ("eb", 0, N * V - 1), ("u", -65535, 65535)):
        if np.min(d[k]) < lo or np.max(d[k]) > hi: bad.append("range of " + k)
    return bad
def reference(x0, l0, ea, eb, u):
    none = N * V
    x = x0.astype(np.int64).reshape(N, 8, 16, V); L = l0.astype(np.int64).reshape(N, 8, 16, V); dr = u.astype(np.int64).reshape(N, 8, 16, RO)
    a = np.stack([gentries(k) for k in ea]).astype(np.int64); b = np.stack([gentries(k) for k in eb]).astype(np.int64)
    for t in range(RO):
        M, tab = tops(x, L); tot = np.add.reduce(tab, axis=1)
        deg = np.add.reduce((L < none).astype(np.int64), axis=2); votes = np.add.reduce((x > M).astype(np.int64), axis=2)
        inv = (deg > 12) | ((deg > 0) & (votes >= 12))
        inv = inv & (np.add.accumulate(inv.astype(np.int64), axis=2) <= H)
        new = np.array(L)
        for g in range(8):
            come = [[] for d in range(N)]
            for q in range(N):
                aa = a[q, g, t * B:(t + 1) * B] + q * V; bb = b[q, g, t * B:(t + 1) * B]; first = tot[g, aa] <= tot[g, bb]
                vs = np.nonzero(inv[q, g])[0]
                rec = np.concatenate([np.where(first, aa, bb), L[q, g][:, vs].T.reshape(-1)])
                giv = np.concatenate([np.where(first, bb, aa), np.repeat(vs + q * V, 16)])
                row = np.concatenate([np.full(B, -1), np.tile(np.arange(16), len(vs))])
                for d in range(N):
                    for s in np.nonzero((rec >= d * V) & (rec < (d + 1) * V))[0][:C]: come[d].append((int(rec[s]) - d * V, int(giv[s]), q, int(row[s])))
            for d in range(N):
                seen = {}
                for v, w, q, i in come[d]:
                    k = seen.get(v, 0); seen[v] = k + 1
                    if k >= A: continue
                    empty = np.nonzero(L[d, g, :, v] == none)[0]
                    if k < len(empty):
                        new[d, g, empty[k], v] = w
                        if i >= 0: new[q, g, i, w - q * V] = none
        x = np.clip(((x + M) >> 1) + dr[..., t:t + 1], 0, 65535); L = new
    return {"yx": x.reshape(N, 128, V).astype(np.float32), "yl": L.reshape(N, 128, V).astype(np.float32)}

@@ -1,0 +1,572 @@
+from concourse.bass import DstId, RemoteDMATransfer
+from concourse.mybir import AluOpType as OP, ActivationFunctionType as AF
+
+N, V, RO = 4, 768, 3
+NONE = N * V
+RQ = 416
+BIG = float(2 ** 22)
+PL = 1056
+DUM = 2881
+F32, B16, I32, U16 = "float32", "bfloat16", "int32", "uint16"
+CUT = 512
+NV = 96
+SCH = [(NV, 128)] + [(a, a + 64) for a in range(128, 704, 64)] + [(704, 736), (736, V)]
+
+
+def _sb(n, d):
+    return ("sbuf", [128, n], d)
+
+
+SCRATCH = {
+    "xi": _sb(V, I32), "li": _sb(V, I32), "eai": _sb(8, I32), "ebi": _sb(8, I32), "ui": _sb(4, I32),
+    "tab0": _sb(3080, F32), "tab1": _sb(3080, F32), "tab2": _sb(3080, F32),
+    "xu": _sb(V, U16), "xo": _sb(V, F32),
+    "xin0": _sb(3 * V, U16), "xin1": _sb(2 * V, U16), "xin2": _sb(2 * V, U16),
+    "Lf": _sb(PL, F32), "L16": _sb(V, U16),
+    "G": _sb(6 * 1024, F32), "Gv": _sb(1024, F32), "MS": _sb(16 * 512, F32), "RP": _sb(1024, B16),
+    "T1": _sb(3104, F32), "T2": _sb(3080, F32), "D": _sb(3144, F32),
+    "lift": _sb(256, B16), "liftG": _sb(512, F32),
+    "I1": _sb(128, F32), "I2": _sb(128, F32), "J16": _sb(256, F32), "pi": _sb(4, I32), "pa": _sb(4, I32),
+    "tmpa": _sb(384, F32), "tmpb": _sb(384, F32),
+    "OBf": _sb(128, F32), "If": _sb(128, F32), "NIf": _sb(128, F32),
+    "OB": _sb(128, B16), "NOB": _sb(128, B16), "OB20": _sb(128, B16), "OB125": _sb(128, B16),
+    "TriEr": _sb(128, B16), "NTriU": _sb(128, B16),
+    "col": _sb(16, F32), "pat": _sb(384, F32),
+    "rp5": _sb(130, F32), "c26": _sb(130, B16), "c25": _sb(256, B16), "ones": _sb(256, B16),
+    "dl": _sb(16, F32), "dl2": _sb(16, F32), "uc": _sb(4, F32),
+    "ea16": _sb(8, U16), "eb16": _sb(8, U16), "af": _sb(8, F32), "bf": _sb(8, F32), "amb": _sb(8, F32),
+    "em": _sb(V, B16), "cl": _sb(V, B16), "gt": _sb(V, B16), "ripe": _sb(800, B16), "cum": _sb(800, B16),
+    "junk": _sb(1280, B16), "cnt": _sb(4, F32), "cs": _sb(2, F32), "vs16": _sb(2, U16),
+    "xa": _sb(32, F32), "dd": _sb(32, F32), "ez": _sb(32, F32), "ef": _sb(2, F32), "et": _sb(2, F32), "gv": _sb(2, F32),
+    "RL": _sb(34, F32), "vsb": _sb(32, F32), "o16": _sb(26, U16), "R16": _sb(26, U16), "giv16": _sb(26, U16),
+    "own": _sb(130, B16), "osc": _sb(130, B16), "oy": _sb(130, F32),
+    "off16": _sb(26, U16), "PA": _sb(RQ, F32), "PB": _sb(RQ, F32), "SW": _sb(5 * RQ, F32),
+    "Pw0": _sb(256, F32), "Pw1": _sb(256, F32), "Pw2": _sb(256, F32),
+    "erT": _sb(776, F32), "wT": _sb(776, F32),
+    "z": _sb(256, F32), "r16": _sb(256, U16), "rl16": _sb(16, U16), "rlf": _sb(16, F32), "rl2": _sb(16, F32),
+    "E": ("sbuf", [128, 16, 256], B16), "Ed": _sb(256, B16),
+    "wg": _sb(256, F32), "erg": _sb(256, F32), "t0": _sb(256, F32), "gm": _sb(256, F32), "mm": _sb(256, F32),
+    "t1": _sb(256, F32), "t2": _sb(256, F32), "t3": _sb(256, F32),
+    "acc": _sb(256, B16), "accW": _sb(5 * RQ, B16),
+    "ka": _sb(16, F32), "kb": _sb(16, F32), "kc": _sb(16, F32), "kd": _sb(16, F32), "od16": _sb(16, U16), "ol16": _sb(16, U16),
+    "lc": _sb(32, F32), "y2": _sb(384, F32), "zz": _sb(384, F32), "clr": _sb(32, F32),
+    "psS": ("psum", [128, 1024], F32), "psD": ("psum", [128, 1024], F32), "psE": ("psum", [128, 1024], F32),
+    "psG": ("psum", [128, 512], F32), "psH": ("psum", [128, 512], F32),
+}
+SEMAPHORES = (["cv", "cs", "ct", "cg", "ld0", "ld1", "ld2", "ld3", "ld4", "ld5", "st0", "st1"]
+              + ["%s%d" % (k, t) for k in ("sx", "sy", "sz", "sp", "sr", "ap", "ar") for t in range(RO)]
+              + ["a%s%d_%d" % (k, t, q) for k in "xy" for t in range(RO) for q in range(N)])
+
+
+def _emit(g, T, ops):
+    queue = {"v": g.vector, "s": g.scalar, "t": g.tensor, "g": g, "y": g.sync}
+    counter = {"v": "cv", "s": "cs", "t": "ct", "g": "cg"}
+    known = {e: {} for e in queue}
+    seq = {e: 0 for e in queue}
+
+    def hit(a, b):
+        return any(x[0] == y[0] and x[1] < y[2] and y[1] < x[2] and (x[3] != y[3] or (x[1] - y[1]) % x[3] == 0)
+                   for x in a for y in b)
+
+    users = {}
+    for i, o in enumerate(ops):
+        e = o["e"]
+        names = set(x[0] for x in o["r"] + o["w"] + o["after"])
+        earlier = sorted(set(j for n in names for j in users.get(n, [])))
+        for n in names:
+            users.setdefault(n, []).append(i)
+        o["waits"] = []
+        o["sig"] = False
+        if e is None:
+            o["key"], o["val"], o["clock"] = ("a", i), 1, {}
+            continue
+        wr = o["w"] + o["after"]
+        pp = [x for x in o["r"] + wr if x[0].startswith("ps")]
+        need = []
+        for p in [ops[j] for j in earlier]:
+            same = p["e"] == e and p["sem"] is None and o["sem"] is None
+            if same and e == "t":
+                continue
+            if hit(o["r"], p["w"]) or hit(wr, p["w"]) or hit(wr, p["r"]) or (not same and hit(pp, p["r"])):
+                need.append(p)
+        for p in reversed(need):
+            if known[e].get(p["key"], 0) >= p["val"]:
+                continue
+            o["waits"].append(p)
+            p["sig"] = True
+            for k, v in list(p["clock"].items()) + [(p["key"], p["val"])]:
+                if known[e].get(k, 0) < v:
+                    known[e][k] = v
+        o["clock"] = dict(known[e])
+        if o["sem"] is None:
+            seq[e] += 1
+            o["key"], o["val"] = e, seq[e]
+        else:
+            o["key"], o["val"] = ("a", i), 1
+    total = {e: 0 for e in counter}
+    for o in ops:
+        if o["sem"] is None and o["sig"]:
+            total[o["e"]] += 1
+            o["sv"] = (counter[o["e"]], total[o["e"]])
+        elif o["sem"] is not None:
+            o["sv"] = o["sem"]
+    seen = {}
+    for o in ops:
+        if o["e"] is None:
+            continue
+        for p in o["waits"]:
+            queue[o["e"]].wait_ge(T.sem[p["sv"][0]], p["sv"][1])
+            seen[p["sv"][0]] = max(seen.get(p["sv"][0], 0), p["sv"][1])
+        ins = o["f"](queue[o["e"]])
+        if o["sem"] is None and o["sig"]:
+            ins.then_inc(T.sem[counter[o["e"]]], 1)
+    for o in ops:
+        if o["sem"] is not None and seen.get(o["sem"][0], 0) < o["sem"][1]:
+            g.wait_ge(T.sem[o["sem"][0]], o["sem"][1])
+
+
+def rank_program(g, core, T, topo):
+    me = T.rank_of(core)
+    if me is None:
+        return
+    ops = []
+
+    def A(name, lo=0, hi=None, step=1):
+        hi = SCRATCH[name][1][1] if hi is None else hi
+        ap = T[name][:, lo:hi] if step == 1 else T[name][:, lo:hi:step]
+        if name.startswith("ps"):
+            lo, hi = lo // 512 * 512, (hi + 511) // 512 * 512
+        return (ap, [(name, lo, hi, step)], [])
+
+    def A3(name, lo, hi, inner):
+        ap = T[name][:, lo, inner] if hi == lo + 1 else T[name][:, lo:hi, inner]
+        return (ap, [(name, lo, hi, 1)], [])
+
+    def X(win, off):
+        return (win[0].indirect(off[0]), win[1], off[1])
+
+    def add(e, f, outs, ins, sem=None, after=()):
+        r, w = [], []
+        for a in ins:
+            if isinstance(a, tuple):
+                r += a[1] + a[2]
+        for a in outs:
+            w += a[1]
+            r += a[2]
+        ops.append({"e": e, "f": f, "r": r, "w": w, "sem": sem, "after": [x for a in after for x in a[1]]})
+
+    def P(a):
+        return a[0] if isinstance(a, tuple) else a
+
+    def cp(o, a):
+        add("v", lambda q: q.tensor_copy(o[0], a[0]), [o], [a])
+
+    def ms(o, c):
+        add("v", lambda q: q.memset(o[0], c), [o], [])
+
+    def tt(o, a, b, op):
+        add("v", lambda q: q.tensor_tensor(o[0], a[0], b[0], op), [o], [a, b])
+
+    def ts(o, a, s1, op0, s2=None, op1=None):
+        if s2 is None:
+            add("v", lambda q: q.tensor_scalar(o[0], a[0], P(s1), None, op0), [o], [a, s1])
+        else:
+            add("v", lambda q: q.tensor_scalar(o[0], a[0], P(s1), P(s2), op0, op1), [o], [a, s1, s2])
+
+    def scan(o, a, b, init, op0, op1):
+        add("v", lambda q: q.tensor_tensor_scan(o[0], a[0], b[0], P(init), op0, op1), [o], [a, b, init])
+
+    def act(o, a, fn, bias=None, scale=None, acc=None):
+        kw = {}
+        if bias is not None:
+            kw["bias"] = P(bias)
+        if scale is not None:
+            kw["scale"] = scale
+        if acc is not None:
+            kw["accum_out"] = acc[0]
+        add("s", lambda q: q.activation(o[0], a[0], fn, **kw), [o] + ([acc] if acc else []), [a, bias])
+
+    def mm(o, l, r, start, stop):
+        add("t", lambda q: q.matmul(o[0], l[0], r[0], start, stop), [o], [l, r])
+
+    def iota(o, pattern, base, cm, whole=False):
+        if whole:
+            add("g", lambda q: q.iota(o[0], pattern, base, cm), [o], [])
+        else:
+            add("g", lambda q: q.iota(o[0], pattern, base, cm, allow_small_or_imprecise_dtypes=True), [o], [])
+
+    def dma(e, o, a, sem):
+        add(e, lambda q: q.dma_start(o[0], a[0]).then_inc(T.sem[sem], 16), [o], [a], sem=(sem, 16))
+
+    def hbm(name):
+        return (T[name][:], [(name, 0, 1, 1)], [])
+
+    others = [q for q in range(N) if q != me]
+    near = [q for q in others if T.cores[q] in topo.cores_of(core)]
+    far = [q for q in others if q not in near]
+    efar = topo.engines(core, T.cores[far[0]])
+    enear = [e for e in topo.engines(core, T.cores[near[0]]) if e not in efar]
+
+    def bits(es):
+        return sum(1 << e for e in es)
+
+    def slot(owner, src):
+        fs = [q for q in range(N) if T.cores[q] not in topo.cores_of(T.cores[owner])]
+        return fs.index(src) if src in fs else len(fs)
+
+    def send(items, sem, after=()):
+        trs = []
+        for q, src, dst, es, rs in items:
+            rid, pid = topo.addr(T.cores[q], core)
+            trs.append(RemoteDMATransfer(dst_ids=[DstId(rid=rid, pnc=pid)], dma_engine_mask=bits(es),
+                                         remote_sem=T.sem[rs], src=src[0], dst=dst))
+        add("g", lambda q: q.remote_dma_fused(trs, local_sem=T.sem[sem]), [], [it[1] for it in items],
+            sem=(sem, sum(len(it[3]) for it in items)), after=after)
+
+    def arrive(outs, sem, n):
+        add(None, None, outs, [], sem=(sem, n))
+
+    h = len(efar) // 2
+    eng = {far[0]: efar[:h], far[1]: efar[h:], near[0]: enear}
+
+    def send_narrow(t, ranks, a, b, tag):
+        xin = "xin%d" % t
+        send([(q, A("xu", a, b), A(xin, slot(q, me) * V + a, slot(q, me) * V + b)[0], eng[q], "a%s%d_%d" % (tag, t, me)) for q in ranks],
+             "s%s%d" % (tag, t))
+        for q in ranks:
+            arrive([A(xin, slot(me, q) * V + a, slot(me, q) * V + b)], "a%s%d_%d" % (tag, t, q), len(eng[q]))
+
+    def send_wide(t):
+        tab, q = "tab%d" % t, near[0]
+        part = A(tab, me * V, (me + 1) * V)
+        send([(q, part, part[0], eng[q], "ax%d_%d" % (t, me))], "sz%d" % t)
+        arrive([A(tab, q * V, (q + 1) * V)], "ax%d_%d" % (t, q), len(eng[q]))
+
+    def widen_x(t, ranks, a, b):
+        for q in ranks:
+            cp(A("tab%d" % t, q * V + a, q * V + b), A("xin%d" % t, slot(me, q) * V + a, slot(me, q) * V + b))
+
+    rcol, rm1, fix, nfix = A("col", 0, 1), A("col", 1, 2), A("col", 2, 3), A("col", 3, 4)
+    b0, b1, fx2, r0 = A("col", 4, 5), A("col", 5, 6), A("col", 6, 7), A("col", 7, 8)
+    TM = A("psG", 256, 512)
+    pat = A("pat", 0, 256)
+
+    HV = V // 2
+    dma("y", A("xi", 0, HV), (T["x0"][:, 0:HV], [], []), "ld0")
+    dma("y", A("xi", HV, V), (T["x0"][:, HV:V], [], []), "ld5")
+    dma("y", A("li"), hbm("l0"), "ld1")
+    dma("y", A("eai", 0, 6), hbm("ea"), "ld2")
+    dma("y", A("ebi", 0, 6), hbm("eb"), "ld3")
+    dma("y", A("ui", 0, 3), hbm("u"), "ld4")
+    iota(A("I2"), [[16, 8], [0, 16]], 0, -1)
+    iota(A("I1"), [[1, 128]], 0, -1)
+    iota(A("pi", 0, 1), [[0, 1]], 0, 1, True)
+    iota(A("J16"), [[0, 16], [1, 16]], 0, 0)
+    iota(A("dl"), [[16, 16]], 0, 0)
+    for t in range(RO):
+        ms(A("tab%d" % t, NONE, 3080), 0.0)
+    ms(A("ones"), 1.0)
+    ms(A("ripe", V, 800), 1.0)
+    ts(A("tmpa", 0, 128), A("I2"), -15.0, OP.max, 0.0, OP.min)
+    ms(A("Lf", V, PL), float(NONE))
+    tt(A("OBf"), A("tmpa", 0, 128), A("I2"), OP.is_equal)
+    ts(A("If"), A("I1"), 0.0, OP.is_equal)
+    ts(A("pa", 0, 1), A("pi", 0, 1), 15, OP.bitwise_and)
+    ts(A("tmpa", 128, 256), A("I1"), 0.0, OP.is_gt)
+    ts(A("tmpa", 256, 384), A("I1"), 0.0, OP.is_lt, -1.0, OP.mult)
+    cp(rcol, A("pa", 0, 1))
+    act(A("OB"), A("OBf"), AF.Copy)
+    act(A("tmpb", 128, 256), A("If"), AF.Copy, scale=-128.0)
+    act(A("z", 0, 128), A("If"), AF.Copy, scale=-4096.0)
+    act(A("NIf"), A("If"), AF.Copy, scale=-1.0)
+    act(A("NOB"), A("OBf"), AF.Copy, scale=-1.0)
+    act(A("OB20"), A("OBf"), AF.Copy, scale=-20.0)
+    act(A("OB125"), A("OBf"), AF.Copy, scale=1.25)
+    tt(A("tmpb", 0, 128), A("tmpa", 128, 256), A("OBf"), OP.mult)
+    tt(A("tmpb", 256, 384), A("tmpa", 256, 384), A("OBf"), OP.mult)
+    cp(A("xu", 0, HV), A("xi", 0, HV))
+    send_narrow(0, others, 0, HV, "x")
+    cp(A("xu", HV, V), A("xi", HV, V))
+    send_narrow(0, others, HV, V, "y")
+    iota(A("lift", 0, NV), [[0, NV // 32], [4096, 32]], 0, 0)
+    iota(A("G", 0, 512), [[4096, 32], [0, 16]], 0, 0)
+    iota(A("T1"), [[1, 3104]], 0, 0)
+    iota(A("T2", 0, NONE), [[0, N], [4096, V]], 0, 0)
+    for k in range(4):
+        act(A("RP", 256 * k, 256 * k + 256), A("J16"), AF.Sign)
+    cp(A("tab0", me * V, (me + 1) * V), A("xi"))
+    tt(A("TriEr"), A("tmpb", 0, 128), A("tmpb", 128, 256), OP.add)
+    tt(A("NTriU"), A("tmpb", 256, 384), A("z", 0, 128), OP.add)
+    ts(r0, rcol, 0.0, OP.is_equal)
+    ts(b0, rcol, -1.0, OP.mult, -0.5, OP.add)
+    ts(b1, rcol, -1.0, OP.mult, -16.5, OP.add)
+    ts(A("t0", 0, 16), A("J16", 0, 16), rcol, OP.is_gt)
+    ts(rm1, r0, 16.0, OP.mult, rcol, OP.add)
+    ts(fix, r0, -2 * BIG, OP.mult, BIG, OP.add)
+    ts(A("y2", 0, 16), A("J16", 0, 16), rcol, OP.is_equal, -BIG, OP.mult)
+    ts(A("dl2"), A("dl"), rcol, OP.add, 800.0, OP.add)
+    ts(rm1, rm1, -1.0, OP.add)
+    ts(nfix, fix, -1.0, OP.mult)
+    ts(fx2, fix, 1.0 / 4096, OP.mult, -0.375, OP.add)
+    ts(A("kd"), A("dl2"), float(DUM - 800), OP.add)
+    ts(A("zz", 0, 16), A("J16", 0, 16), rm1, OP.is_equal, 2 * BIG, OP.mult)
+    ms(A("c25"), 2.5 / 16)
+    tt(A("pat", 0, 16), A("y2", 0, 16), A("zz", 0, 16), OP.add)
+    for n in (16, 32, 64, 128):
+        act(A("pat", n, 2 * n), A("pat", 0, n), AF.Copy)
+        act(A("t0", n, 2 * n), A("t0", 0, n), AF.Copy)
+    act(A("pat", 256, 384), A("pat", 0, 128), AF.Copy)
+    act(TM, A("t0"), AF.Copy)
+    act(A("liftG"), A("G", 0, 512), AF.Copy, scale=16.0)
+    for k in range(0, 5 * RQ, 1024):
+        n = min(1024, 5 * RQ - k)
+        act(A("accW", k, k + n), A("RP", 0, n), AF.Copy, scale=0.0)
+    cp(A("L16"), A("li"))
+    ms(A("lift", NV, 256), 0.0)
+    cp(A("Lf", 0, V), A("li"))
+    ms(A("rp5"), 0.0)
+    for d in range(5):
+        ms(A("c26", d, 130, 5), (RQ * d + 4096) / 16.0)
+    ts(A("rp5", 0, 130, 5), A("rp5", 0, 130, 5), 16384.0, OP.add)
+    cp(A("dl"), A("kd"))
+    ms(A("T2", NONE, 3080), 0.0)
+    ms(A("erT", V, 776), 0.0)
+    ms(A("wT", V, 776), 2.5)
+    ms(A("clr", 24, 32), 0.0)
+    ts(A("af", 0, 6), A("eai", 0, 6), float(me * V), OP.add)
+    cp(A("bf", 0, 6), A("ebi", 0, 6))
+    cp(A("eb16", 0, 6), A("ebi", 0, 6))
+    ts(A("uc", 0, 3), A("ui", 0, 3), -0.25, OP.add)
+    cp(A("ea16", 0, 6), A("af", 0, 6))
+    tt(A("amb", 0, 6), A("af", 0, 6), A("bf", 0, 6), OP.subtract)
+    ts(A("em"), A("L16"), float(NONE), OP.is_equal)
+    widen_x(0, near + far, 0, HV)
+    widen_x(0, near + far, HV, V)
+
+    for t in range(RO):
+        tab = A("tab%d" % t)
+        last = t == RO - 1
+        e2 = (2 * t, 2 * t + 2)
+
+        def x(a, b):
+            return A("tab%d" % t, me * V + a, me * V + b)
+
+        def gslot(c):
+            return A("G", 1024 * (c % 6), 1024 * (c % 6) + 16 * (SCH[c][1] - SCH[c][0]))
+
+        def gather(c):
+            act(gslot(c), X(tab, A("L16", *SCH[c])), AF.Copy)
+
+        def fold(c):
+            a, b = SCH[c]
+            scan(A("MS", 16 * (a % 512), 16 * (a % 512 + b - a)), A("RP", 0, 16 * (b - a)), gslot(c), 0.0, OP.mult, OP.max)
+            if c + 6 < len(SCH):
+                gather(c + 6)
+
+        def own_gather(k):
+            tt(A("Gv", 512 * (k % 2), 512 * (k % 2) + 512), X(tab, A("L16", 32 * k, 32 * k + 32)), A("liftG"), OP.add)
+
+        def own_fold(k):
+            o = 512 * (k % 2)
+            scan(A("MS", 512 * k + 1, 512 * k + 512, 2), A("Gv", o, o + 512, 2), A("Gv", o + 1, o + 512, 2), 0.0, OP.max, OP.max)
+
+        def M(a, b):
+            return A("MS", 16 * (a % 512) + 15, 16 * (a % 512 + b - a), 16)
+
+        def diff_open(a, b):
+            mm(A("psD", a, b), A("If"), x(a, b), True, False)
+            if a == 0:
+                mm(A("psD", a, b), A("OB"), A("lift", a, b), False, False)
+
+        def diff_close(a, b):
+            mm(A("psD", a, b), A("NIf"), M(a, b), False, True)
+
+        def score_open(a, b):
+            mm(A("psE", a, b), A("OB20"), A("em", a, b), True, False)
+            mm(A("psE", a, b), A("OB125"), A("cl", a, b), False, False)
+
+        def total_open():
+            mm(A("psS", 0, 512), A("If"), x(0, 512), True, False)
+            mm(A("psS", 0, 256), A("NOB"), A("lift"), False, False)
+            mm(A("psS", 512, V), A("If"), x(512, V), True, False)
+
+        def total(a, b):
+            mm(A("psS", a, b), A("If"), M(a, b), False, a > 0)
+
+        def votes(a, b):
+            ts(A("gt", a, b), A("psD", a, b), 0.5, OP.is_gt)
+            mm(A("psE", a, b), A("OB"), A("gt", a, b), False, True)
+
+        def ripe(a, b):
+            ts(A("ripe", a, b), A("psE", a, b), 12.0, OP.is_ge)
+
+        def count(a, b):
+            scan(A("cum", a, b), A("ones", 0, b - a), A("ripe", a, b), A("cum", a - 1, a) if a else 0.0, OP.mult, OP.add)
+
+        def new_x(a, b):
+            ts(A("xu", a, b), A("psS", a, b), 0.5, OP.mult, A("uc", t, t + 1), OP.add)
+
+        def empties(ps, l):
+            mm(A(ps, 0, 512), A(l), A("em", 0, 512), True, True)
+            mm(A(ps, 512, V), A(l), A("em", 512, V), True, True)
+
+        iota(A("D", 0, 2 * PL + 776), [[0, 2 * PL + 776]], 0, 0)
+        diff_open(0, 256)
+        diff_open(512, 640)
+        total_open()
+        for c in range(6):
+            gather(c)
+        own_gather(0)
+        if t:
+            ts(A("em"), A("L16"), float(NONE), OP.is_equal)
+        empties("psE", "OB")
+        own_fold(0)
+        fold(0)
+        cp(A("xa"), X(tab, A("ea16", *e2)))
+        ts(A("cl"), A("psE", 0, V), 4.0, OP.max, 15.0, OP.min)
+        tt(A("dd"), X(tab, A("eb16", *e2)), A("xa"), OP.subtract)
+        mm(A("psG", 160, 192), A("OBf"), A("dd"), True, True)
+        score_open(0, 256)
+        score_open(512, 640)
+        fold(1)
+        own_gather(1)
+        scan(A("ez"), A("psG", 160, 192), A("pat", 0, 32), nfix, OP.min, OP.add)
+        own_fold(1)
+        ts(A("ef"), A("ez", 15, 32, 16), fix, OP.add, 0.0, OP.is_ge)
+        fold(2)
+        tt(A("et"), A("ef"), A("amb", *e2), OP.mult)
+        own_gather(2)
+        tt(A("RL", 0, 2), A("et"), A("bf", *e2), OP.add)
+        tt(A("gv"), A("af", *e2), A("et"), OP.subtract)
+        own_fold(2)
+        diff_close(0, 256)
+        fold(3)
+        cp(A("giv16", 0, 2), A("gv"))
+        votes(0, 256)
+        total(0, 256)
+        diff_open(256, 512)
+        fold(4)
+        ripe(0, 256)
+        score_open(256, 512)
+        for d in range(4):
+            ms(A("SW", RQ * d, RQ * d + 64), 4096.0 * V)
+        count(0, 256)
+        fold(5)
+        fold(6)
+        diff_close(256, 512)
+        fold(7)
+        votes(256, 512)
+        total(256, 512)
+        fold(8)
+        diff_close(512, 640)
+        ripe(256, 512)
+        if not last:
+            new_x(0, CUT)
+            send_narrow(t + 1, far, 0, CUT, "x")
+        count(256, 512)
+        votes(512, 640)
+        fold(9)
+        ripe(512, 640)
+        score_open(640, V)
+        count(512, 640)
+        fold(10)
+        act(A("junk", 0, 640), A("cum", 0, 640), AF.Sign, bias=b0, acc=A("cnt", 0, 1))
+        act(A("junk", 640, 1280), A("cum", 0, 640), AF.Sign, bias=b1, acc=A("cnt", 1, 2))
+        fold(11)
+        tt(A("gt", 640, V), x(640, V), M(640, V), OP.is_gt)
+        mm(A("psE", 640, V), A("OB"), A("gt", 640, V), False, True)
+        ripe(640, V)
+        count(640, 800)
+        act(A("junk", 0, 160), A("cum", 640, 800), AF.Sign, bias=b0, acc=A("cnt", 2, 3))
+        act(A("junk", 160, 320), A("cum", 640, 800), AF.Sign, bias=b1, acc=A("cnt", 3, 4))
+        ts(A("cs"), A("cnt", 0, 2), -0.5, OP.mult, 400.0, OP.add)
+        for c in range(2):
+            ts(A("vs16", c, c + 1), A("cnt", 2 + c, 3 + c), -0.5, OP.mult, A("cs", c, c + 1), OP.add)
+
+        mm(A("psG", 0, 130), A("OB"), A("c26"), True, False)
+        cp(A("RL", 2, 34), X(A("Lf", 0, 800), A("vs16")))
+        cp(A("vsb"), X(A("T1", me * V, me * V + 800), A("vs16")))
+        ts(A("o16"), A("RL", 0, 26), 1.0 / V, OP.mult, -0.4995, OP.add)
+        cp(A("R16"), A("RL", 0, 26))
+        cp(A("giv16", 2, 26), A("vsb", 0, 24))
+        act(A("PA"), X(A("T2"), A("R16")), AF.Copy)
+        act(A("PB"), X(A("T1"), A("giv16")), AF.Identity, bias=float(NONE), scale=-1.0)
+        for d in range(5):
+            ts(A("own", d, 130, 5), A("o16"), float(d), OP.is_equal)
+        mm(A("psG", 0, 130), A("NTriU"), A("own"), False, False)
+        for d in range(5):
+            scan(A("osc", d, 130, 5), A("ones", 0, 26), A("own", d, 130, 5), 0.0, OP.mult, OP.add)
+        mm(A("psG", 0, 130), A("OB"), A("osc"), False, True)
+        total(512, V)
+        empties("psE", "OB")
+        empties("psD", "TriEr")
+        scan(A("oy"), A("rp5"), A("psG", 0, 130), 0.0, OP.add, OP.min)
+        ts(A("off16"), A("oy", 4, 130, 5), -1.0, OP.add)
+        tt(X(A("SW"), A("off16")), A("PA"), A("PB"), OP.add)
+        Pw = "Pw%d" % t
+        send([(q, A("SW", RQ * q, RQ * q + 64), A(Pw, 64 * me, 64 * me + 64)[0], eng[q], "ap%d" % t) for q in others],
+             "sp%d" % t, after=[A("accW")])
+        arrive([A(Pw, 64 * q, 64 * q + 64) for q in others], "ap%d" % t, 2 * h + len(enear))
+        act(A("wT", 0, V), A("psE", 0, V), AF.Relu, bias=2.5, scale=-1.0)
+        act(A("erT", 0, V), A("psD", 0, V), AF.Relu, bias=-125.5, scale=-1.0)
+        new_x(0 if last else CUT, V)
+        cp(A(Pw, 64 * me, 64 * me + 64), A("SW", RQ * me, RQ * me + 64))
+        if last:
+            cp(A("xo"), A("xu"))
+            dma("y", hbm("yx"), A("xo"), "st0")
+        else:
+            send_narrow(t + 1, far, CUT, V, "y")
+            cp(A("tab%d" % (t + 1), me * V, (me + 1) * V), A("xu"))
+            send_wide(t + 1)
+            widen_x(t + 1, far, 0, CUT)
+
+        mm(A("psH", 0, 256), A("OB"), A("c25"), True, False)
+        scan(A("z"), A(Pw), pat, nfix, OP.min, OP.add)
+        ts(A("r16"), A(Pw), 1.0 / 4096, OP.mult, -0.375, OP.add)
+        ts(A("rl16"), A("z", 15, 256, 16), 1.0 / 4096, OP.mult, fx2, OP.add)
+        cp(A("rlf"), A("rl16"))
+        act(A("wg"), X(A("wT"), A("rl16")), AF.Copy)
+        act(A("erg"), X(A("erT"), A("rl16")), AF.Copy)
+        act(A("t0"), X(A("Lf", 0, 776), A("rl16")), AF.Copy)
+        for c in range(16):
+            ts(A3("E", c, c + 1, slice(0, 256 - 16 * c)), A("r16", 16 * c, 256), A("rlf", c, c + 1), OP.is_equal)
+            if c < 15:
+                mm(A("psH", 16 * c + 16, 256), A("NOB"), A3("E", c, c + 1, slice(16, 256 - 16 * c)), False, False)
+        tt(A("Ed"), A3("E", 0, 16, slice(0, 16)), TM, OP.mult)
+        mm(A("psH", 0, 256), A("NOB"), A("Ed"), False, True)
+        tt(A("gm"), X(A("T2", 0, 776), A("rl16")), A(Pw), OP.subtract)
+        tt(A("acc"), A("psH", 0, 256), A("wg"), OP.is_gt)
+        send([(q, A("acc", 64 * q, 64 * q + 64), A("accW", RQ * me, RQ * me + 64)[0], eng[q], "ar%d" % t) for q in others], "sr%d" % t)
+        arrive([A("accW", RQ * q, RQ * q + 64) for q in others], "ar%d" % t, 2 * h + len(enear))
+        act(A("accW", RQ * me, RQ * me + 64), A("acc", 64 * me, 64 * me + 64), AF.Copy)
+
+        scan(A("z"), A("psH", 0, 256), pat, nfix, OP.min, OP.add)
+        ts(A("rl2"), A("rlf"), 2.5 * PL, OP.add)
+        ts(A("ka"), A("z", 15, 256, 16), fix, OP.add, -float(PL), OP.mult)
+        tt(A("mm"), A("psH", 0, 256), A("erg"), OP.is_equal)
+        tt(A("kb"), A("ka"), A("rl2"), OP.add)
+        tt(A("kc"), A("kb"), A("dl"), OP.min)
+        tt(A("kd"), A("kb"), A("dl2"), OP.min)
+        cp(A("od16"), A("kc"))
+        cp(A("ol16"), A("kd"))
+        tt(X(A("D"), A("od16")), A("mm"), A("gm"), OP.mult)
+        act(A("t3"), X(A("D", 2 * PL, 2 * PL + 776), A("rl16")), AF.Copy)
+        act(A("y2"), X(A("accW"), A("off16", 2, 26)), AF.Copy)
+        tt(A("t1"), X(A("D", 0, 776), A("rl16")), A("t0"), OP.add)
+        tt(A("t2"), X(A("D", PL, PL + 776), A("rl16")), A("t1"), OP.add)
+        tt(X(A("Lf"), A("ol16")), A("t2"), A("t3"), OP.add)
+        if not last:
+            widen_x(t + 1, far[:1], CUT, V)
+        cp(A("lc"), X(A("Lf", 0, 800), A("vs16")))
+        if not last:
+            widen_x(t + 1, far[1:], CUT, V)
+        scan(A("zz"), A("y2"), A("pat"), nfix, OP.min, OP.add)
+        ts(A("clr", 0, 24), A("zz", 15, 384, 16), fix, OP.add, float(NONE), OP.mult)
+        tt(X(A("Lf", 0, 800), A("vs16")), A("lc"), A("clr"), OP.max)
+        if last:
+            dma("y", hbm("yl"), A("Lf", 0, V), "st1")
+        else:
+            cp(A("L16", NV, 192), A("Lf", NV, 192))
+            cp(A("L16", 0, NV), A("Lf", 0, NV))
+            cp(A("L16", 192, V), A("Lf", 192, V))
+    _emit(g, T, ops)

@@ -5,12 +5,26 @@ N, V, RO = 4, 768, 3
 NONE = N * V
 RQ = 416
 BIG = float(2 ** 22)
-PL = 1056
-DUM = 2881
+SP = 800
+WN = 808
+PL = 1064
+DUM = 2936
+DQ = 4 * WN
 F32, B16, I32, U16 = "float32", "bfloat16", "int32", "uint16"
-CUT = 512
-NV = 96
-SCH = [(NV, 128)] + [(a, a + 64) for a in range(128, 704, 64)] + [(704, 736), (736, V)]
+EARLY = 512
+LAST = 704
+BLOCKS = [(0, 256), (256, 512), (512, LAST), (LAST, V)]
+PIECES = [(0, 512), (512, V)]
+WIDE = [True, False]
+OPENING = [(0, 256), (256, V)]
+OWN = 128
+GS = 7
+RIPE = ["sssv", "sssv", "sssv"]
+CY, VC, SCALL, GA, SC, PE, SYNC, HOP, FIRST = 0.83, 55.0, 150.0, 1.75, 3.8, 0.7, 100.0, 700.0, 1800.0
+FOLD = 1024
+ROW, RATE, PORT = 35.0, 30.0, 100.0
+TURNS = 4000
+PLANS = {}
 
 
 def _sb(n, d):
@@ -19,43 +33,136 @@ def _sb(n, d):
 
 SCRATCH = {
     "xi": _sb(V, I32), "li": _sb(V, I32), "eai": _sb(8, I32), "ebi": _sb(8, I32), "ui": _sb(4, I32),
-    "tab0": _sb(3080, F32), "tab1": _sb(3080, F32), "tab2": _sb(3080, F32),
-    "xu": _sb(V, U16), "xo": _sb(V, F32),
-    "xin0": _sb(3 * V, U16), "xin1": _sb(2 * V, U16), "xin2": _sb(2 * V, U16),
-    "Lf": _sb(PL, F32), "L16": _sb(V, U16),
-    "G": _sb(6 * 1024, F32), "Gv": _sb(1024, F32), "MS": _sb(16 * 512, F32), "RP": _sb(1024, B16),
-    "T1": _sb(3104, F32), "T2": _sb(3080, F32), "D": _sb(3144, F32),
-    "lift": _sb(256, B16), "liftG": _sb(512, F32),
-    "I1": _sb(128, F32), "I2": _sb(128, F32), "J16": _sb(256, F32), "pi": _sb(4, I32), "pa": _sb(4, I32),
-    "tmpa": _sb(384, F32), "tmpb": _sb(384, F32),
-    "OBf": _sb(128, F32), "If": _sb(128, F32), "NIf": _sb(128, F32),
-    "OB": _sb(128, B16), "NOB": _sb(128, B16), "OB20": _sb(128, B16), "OB125": _sb(128, B16),
+    "tab0": _sb(3080, F32), "tab1": _sb(3080, F32),
+    "xu": _sb(V, U16), "xin": _sb(6 * V, U16),
+    "Lf": _sb(PL, F32), "L16": _sb(V, U16), "Lx16": _sb(32, U16),
+    "G": _sb(1024 * GS, F32), "MS": _sb(4096, F32),
+    "Q": _sb(2 * EARLY, F32), "Mx": _sb(512, F32), "RP": _sb(FOLD, B16),
+    "T1": _sb(3104, F32), "T3": _sb(WN, F32),
+    "D0": _sb(DQ + 256, F32), "D1": _sb(DQ + 256, F32), "F": _sb(4 * EARLY + DQ + 256, F32),
+    "out0": _sb(800, B16), "out1": _sb(800, B16), "kill": _sb(32, B16),
+    "lift": _sb(256, B16), "ramp": _sb(512, B16), "liftG": _sb(512, F32),
+    "pi": _sb(4, I32), "pa": _sb(4, I32),
+    "OBf": _sb(128, F32), "If": _sb(128, F32), "Hf": _sb(128, F32),
+    "NOH": _sb(128, B16), "OB": _sb(128, B16), "NOB": _sb(128, B16), "OB40": _sb(128, B16),
     "TriEr": _sb(128, B16), "NTriU": _sb(128, B16),
-    "col": _sb(16, F32), "pat": _sb(384, F32),
-    "rp5": _sb(130, F32), "c26": _sb(130, B16), "c25": _sb(256, B16), "ones": _sb(256, B16),
-    "dl": _sb(16, F32), "dl2": _sb(16, F32), "uc": _sb(4, F32),
+    "col": _sb(20, F32), "pat": _sb(384, F32),
+    "rp5": _sb(130, F32), "r26": _sb(130, B16), "c26": _sb(130, B16), "c25": _sb(256, B16), "ones": _sb(256, B16),
+    "nil": _sb(256, B16), "dl": _sb(48, F32), "uc": _sb(4, F32),
     "ea16": _sb(8, U16), "eb16": _sb(8, U16), "af": _sb(8, F32), "bf": _sb(8, F32), "amb": _sb(8, F32),
-    "em": _sb(V, B16), "cl": _sb(V, B16), "gt": _sb(V, B16), "ripe": _sb(800, B16), "cum": _sb(800, B16),
-    "junk": _sb(1280, B16), "cnt": _sb(4, F32), "cs": _sb(2, F32), "vs16": _sb(2, U16),
+    "em": _sb(800, B16), "cl": _sb(V, B16), "gt": _sb(800, B16), "ripe": _sb(800, B16), "cum": _sb(800, B16),
+    "cnt": _sb(8, F32), "cs": _sb(2, F32), "vs16": _sb(2, U16),
     "xa": _sb(32, F32), "dd": _sb(32, F32), "ez": _sb(32, F32), "ef": _sb(2, F32), "et": _sb(2, F32), "gv": _sb(2, F32),
     "RL": _sb(34, F32), "vsb": _sb(32, F32), "o16": _sb(26, U16), "R16": _sb(26, U16), "giv16": _sb(26, U16),
     "own": _sb(130, B16), "osc": _sb(130, B16), "oy": _sb(130, F32),
     "off16": _sb(26, U16), "PA": _sb(RQ, F32), "PB": _sb(RQ, F32), "SW": _sb(5 * RQ, F32),
-    "Pw0": _sb(256, F32), "Pw1": _sb(256, F32), "Pw2": _sb(256, F32),
-    "erT": _sb(776, F32), "wT": _sb(776, F32),
-    "z": _sb(256, F32), "r16": _sb(256, U16), "rl16": _sb(16, U16), "rlf": _sb(16, F32), "rl2": _sb(16, F32),
-    "E": ("sbuf", [128, 16, 256], B16), "Ed": _sb(256, B16),
+    "Pw0": _sb(256, F32), "Pw1": _sb(256, F32),
+    "z": _sb(256, F32), "z2": _sb(256, F32), "r16": _sb(256, U16), "rl16": _sb(16, U16), "rlf": _sb(16, F32),
+    "E": ("sbuf", [128, 16, 256], B16), "Ed": _sb(256, B16), "TM": _sb(256, B16), "emr": _sb(256, B16),
     "wg": _sb(256, F32), "erg": _sb(256, F32), "t0": _sb(256, F32), "gm": _sb(256, F32), "mm": _sb(256, F32),
-    "t1": _sb(256, F32), "t2": _sb(256, F32), "t3": _sb(256, F32),
-    "acc": _sb(256, B16), "accW": _sb(5 * RQ, B16),
-    "ka": _sb(16, F32), "kb": _sb(16, F32), "kc": _sb(16, F32), "kd": _sb(16, F32), "od16": _sb(16, U16), "ol16": _sb(16, U16),
-    "lc": _sb(32, F32), "y2": _sb(384, F32), "zz": _sb(384, F32), "clr": _sb(32, F32),
+    "acc": _sb(256, F32), "accW": _sb(5 * RQ, F32),
+    "k": _sb(256, F32), "od16": _sb(16, U16), "ol16": _sb(16, U16), "of16": _sb(16, U16), "w16": _sb(16, U16),
+    "p16": _sb(8, U16), "liftx": _sb(32, F32),
+    "lc": _sb(128, F32), "clr": _sb(32, F32),
     "psS": ("psum", [128, 1024], F32), "psD": ("psum", [128, 1024], F32), "psE": ("psum", [128, 1024], F32),
     "psG": ("psum", [128, 512], F32), "psH": ("psum", [128, 512], F32),
 }
-SEMAPHORES = (["cv", "cs", "ct", "cg", "ld0", "ld1", "ld2", "ld3", "ld4", "ld5", "st0", "st1"]
-              + ["%s%d" % (k, t) for k in ("sx", "sy", "sz", "sp", "sr", "ap", "ar") for t in range(RO)]
-              + ["a%s%d_%d" % (k, t, q) for k in "xy" for t in range(RO) for q in range(N)])
+SEMAPHORES = (["cv", "cs", "ct", "cg", "lx0", "lx1", "lx2", "ld1", "ld2", "ld3", "ld4", "st0", "st1", "sn", "an", "ah1", "ah2"]
+              + ["%s%d" % (k, t) for k in ("sp", "sr", "ap", "ar") for t in range(RO)]
+              + ["sx%d_%d" % (t, c) for t in range(RO) for c in range(3)]
+              + ["ax%d_%d_%d" % (t, c, q) for t in range(RO) for c in range(3) for q in range(N)])
+
+
+def _hit(a, b):
+    return any(x[0] == y[0] and x[1] < y[2] and y[1] < x[2] and (x[3] != y[3] or (x[1] - y[1]) % x[3] == 0)
+               for x in a for y in b)
+
+
+def _needs(ops):
+    users = {}
+    for i, o in enumerate(ops):
+        names = set(x[0] for x in o["r"] + o["w"] + o["after"])
+        earlier = sorted(set(j for n in names for j in users.get(n, [])))
+        for n in names:
+            users.setdefault(n, []).append(i)
+        wr = o["w"] + o["after"]
+        pp = [x for x in o["r"] + wr if x[0].startswith("ps")]
+        o["need"], o["past"] = set(), 0
+        for j in reversed(earlier):
+            p = ops[j]
+            if not o["past"] >> j & 1 and (_hit(o["r"], p["w"]) or _hit(wr, p["w"]) or _hit(wr, p["r"]) or _hit(pp, p["r"])):
+                o["need"].add(j)
+                o["past"] |= p["past"] | 1 << j
+
+
+def _order(ops):
+    n = len(ops)
+    pre, suc = [[] for _ in ops], [[] for _ in ops]
+    for i, o in enumerate(ops):
+        o["pre"] = sorted(o["need"] | set(o["behind"]))
+        for j in o["pre"]:
+            gap = 0.0 if ops[j]["e"] == o["e"] == "t" else SYNC + ops[j]["fly"]
+            if o["f"] and j not in o["need"]:
+                gap = 0.0
+            pre[i].append((j, gap))
+            suc[j].append((i, gap))
+    hold, eng = [o["hold"] for o in ops], [o["e"] for o in ops]
+    shape = tuple(hold)
+    if shape in PLANS:
+        at = dict((i, k) for k, i in enumerate(PLANS[shape]))
+        if all(at[j] < at[i] for i in range(n) for j, gap in pre[i]):
+            return PLANS[shape]
+
+    def place(key, pre, way):
+        key = list(key)
+        for i in range(n)[::way]:
+            for j, gap in pre[i]:
+                if key[j] > key[i]:
+                    key[i] = key[j]
+        start, begin, finish = [0.0] * n, {}, {}
+        for i in sorted(range(n)[::way], key=lambda i: key[i]):
+            at, d = 0.0, hold[i]
+            for j, gap in pre[i]:
+                if start[j] + hold[j] + gap > at:
+                    at = start[j] + hold[j] + gap
+            if eng[i]:
+                b, f = begin.setdefault(eng[i], []), finish.setdefault(eng[i], [])
+                k, hi = 0, len(f)
+                while k < hi:
+                    if f[(k + hi) // 2] > at:
+                        hi = (k + hi) // 2
+                    else:
+                        k = (k + hi) // 2 + 1
+                while k < len(b) and b[k] < at + d - 1e-6:
+                    at = max(at, f[k])
+                    k += 1
+                b.insert(k, at)
+                f.insert(k, at + d)
+            start[i] = at
+        return start
+
+    def tighten(start):
+        late = place([-start[i] - hold[i] for i in range(n)], suc, -1)
+        start = place([-late[i] - hold[i] for i in range(n)], pre, 1)
+        return max(start[i] + hold[i] for i in range(n)), start
+
+    seed = [1]
+
+    def chance():
+        seed[0] = (seed[0] * 1103515245 + 12345) % 2 ** 31
+        return seed[0] / 2.0 ** 31
+
+    best = now = tighten(place(range(n), pre, 1))
+    for turn in range(TURNS):
+        by, mid, far = 300 + 1200 * chance(), now[0] * chance(), 5000 + 25000 * chance()
+        new = tighten(place([s + by * (2 * chance() - 1) if abs(s - mid) < far else s for s in now[1]], pre, 1))
+        if new[0] <= now[0] + 100:
+            now = new
+        if new[0] < best[0]:
+            best = new
+    PLANS[shape] = sorted(range(n), key=lambda i: (best[1][i], i))
+    PLANS["end"] = best[0]
+    return PLANS[shape]
 
 
 def _emit(g, T, ops):
@@ -63,33 +170,21 @@ def _emit(g, T, ops):
     counter = {"v": "cv", "s": "cs", "t": "ct", "g": "cg"}
     known = {e: {} for e in queue}
     seq = {e: 0 for e in queue}
-
-    def hit(a, b):
-        return any(x[0] == y[0] and x[1] < y[2] and y[1] < x[2] and (x[3] != y[3] or (x[1] - y[1]) % x[3] == 0)
-                   for x in a for y in b)
-
-    users = {}
-    for i, o in enumerate(ops):
+    _needs(ops)
+    order = _order(ops)
+    place = dict((i, k) for k, i in enumerate(order))
+    for i in order:
+        o = ops[i]
         e = o["e"]
-        names = set(x[0] for x in o["r"] + o["w"] + o["after"])
-        earlier = sorted(set(j for n in names for j in users.get(n, [])))
-        for n in names:
-            users.setdefault(n, []).append(i)
         o["waits"] = []
         o["sig"] = False
-        if e is None:
+        if o["f"] is None:
             o["key"], o["val"], o["clock"] = ("a", i), 1, {}
             continue
-        wr = o["w"] + o["after"]
-        pp = [x for x in o["r"] + wr if x[0].startswith("ps")]
-        need = []
-        for p in [ops[j] for j in earlier]:
-            same = p["e"] == e and p["sem"] is None and o["sem"] is None
-            if same and e == "t":
-                continue
-            if hit(o["r"], p["w"]) or hit(wr, p["w"]) or hit(wr, p["r"]) or (not same and hit(pp, p["r"])):
-                need.append(p)
-        for p in reversed(need):
+        for p in [ops[j] for j in sorted(o["need"], key=lambda j: -place[j])]:
+            if p["e"] == e and p["sem"] is None and o["sem"] is None:
+                if e == "t" or not (_hit(o["r"], p["w"]) or _hit(o["w"], p["w"] + p["r"])):
+                    continue
             if known[e].get(p["key"], 0) >= p["val"]:
                 continue
             o["waits"].append(p)
@@ -103,6 +198,7 @@ def _emit(g, T, ops):
             o["key"], o["val"] = e, seq[e]
         else:
             o["key"], o["val"] = ("a", i), 1
+    ops = [ops[i] for i in order]
     total = {e: 0 for e in counter}
     for o in ops:
         if o["sem"] is None and o["sig"]:
@@ -112,7 +208,7 @@ def _emit(g, T, ops):
             o["sv"] = o["sem"]
     seen = {}
     for o in ops:
-        if o["e"] is None:
+        if o["f"] is None:
             continue
         for p in o["waits"]:
             queue[o["e"]].wait_ge(T.sem[p["sv"][0]], p["sv"][1])
@@ -125,27 +221,55 @@ def _emit(g, T, ops):
             g.wait_ge(T.sem[o["sem"][0]], o["sem"][1])
 
 
+def _helper(q, T, topo):
+    far = [c for c in T.cores if c not in topo.cores_of(T.cores[q])]
+    return [c for c in topo.cores_of(far[0]) if c not in T.cores and topo.die(c) == topo.die(T.cores[q])][0]
+
+
+def _hand_on(g, core, q, T, topo):
+    here = [c for c in T.cores if c in topo.cores_of(core)]
+    for t in range(1, RO):
+        for c, (a, b) in enumerate(PIECES):
+            if WIDE[c]:
+                part = T["tab%d" % (t % 2)][:, q * V + a:q * V + b]
+                g.wait_ge(T.sem["ah%d" % t], len(topo.engines(T.cores[q], core)))
+                trs = []
+                for k, dst in enumerate(here):
+                    rid, pid = topo.addr(dst, core)
+                    es = topo.engines(core, dst)
+                    es = es[len(es) // 2 * k:len(es) // 2 * (k + 1)]
+                    trs.append(RemoteDMATransfer(dst_ids=[DstId(rid=rid, pnc=pid)], dma_engine_mask=sum(1 << e for e in es),
+                                                 remote_sem=T.sem["ax%d_%d_%d" % (t, c, q)], src=part, dst=part))
+                g.remote_dma_fused(trs, local_sem=T.sem["sx%d_%d" % (t, c)])
+                g.wait_ge(T.sem["sx%d_%d" % (t, c)], 2 * len(es))
+
+
 def rank_program(g, core, T, topo):
     me = T.rank_of(core)
     if me is None:
+        for q in range(N):
+            if core == _helper(q, T, topo):
+                _hand_on(g, core, q, T, topo)
         return
     ops = []
+    sends, moves = [], []
 
     def A(name, lo=0, hi=None, step=1):
         hi = SCRATCH[name][1][1] if hi is None else hi
         ap = T[name][:, lo:hi] if step == 1 else T[name][:, lo:hi:step]
+        n = (hi - lo + step - 1) // step
         if name.startswith("ps"):
-            lo, hi = lo // 512 * 512, (hi + 511) // 512 * 512
-        return (ap, [(name, lo, hi, step)], [])
+            lo, hi, step = lo // 512 * 512, (hi + 511) // 512 * 512, 1
+        return (ap, [(name, lo, hi, step)], [], n, 2 if SCRATCH[name][2] in (B16, U16) else 4, name.startswith("ps"))
 
-    def A3(name, lo, hi, inner):
-        ap = T[name][:, lo, inner] if hi == lo + 1 else T[name][:, lo:hi, inner]
-        return (ap, [(name, lo, hi, 1)], [])
+    def A3(name, lo, hi, a, b):
+        ap = T[name][:, lo, a:b] if hi == lo + 1 else T[name][:, lo:hi, a:b]
+        return (ap, [(name, lo, hi, 1)], [], (hi - lo) * (b - a), 2, False)
 
     def X(win, off):
-        return (win[0].indirect(off[0]), win[1], off[1])
+        return (win[0].indirect(off[0]), win[1], off[1], 16 * off[3], 4, False)
 
-    def add(e, f, outs, ins, sem=None, after=()):
+    def add(e, f, hold, fly, outs, ins, sem=None, after=(), behind=()):
         r, w = [], []
         for a in ins:
             if isinstance(a, tuple):
@@ -153,53 +277,63 @@ def rank_program(g, core, T, topo):
         for a in outs:
             w += a[1]
             r += a[2]
-        ops.append({"e": e, "f": f, "r": r, "w": w, "sem": sem, "after": [x for a in after for x in a[1]]})
+        ops.append({"e": e, "f": f, "hold": hold, "fly": fly, "r": r, "w": w, "sem": sem,
+                    "after": [x for a in after for x in a[1]], "behind": list(behind)})
 
     def P(a):
         return a[0] if isinstance(a, tuple) else a
 
+    def vtime(o, ins, k=1.0):
+        if o[2]:
+            return 50 + SC * CY * o[3]
+        if ins and ins[0][2]:
+            return 50 + GA * CY * o[3]
+        return VC + CY * k * o[3] * (0.5 if all(a[4] == 2 for a in [o] + ins) else 1)
+
     def cp(o, a):
-        add("v", lambda q: q.tensor_copy(o[0], a[0]), [o], [a])
+        add("v", lambda q: q.tensor_copy(o[0], a[0]), vtime(o, [a]), 0, [o], [a])
 
     def ms(o, c):
-        add("v", lambda q: q.memset(o[0], c), [o], [])
+        add("v", lambda q: q.memset(o[0], c), vtime(o, []), 0, [o], [])
 
     def tt(o, a, b, op):
-        add("v", lambda q: q.tensor_tensor(o[0], a[0], b[0], op), [o], [a, b])
+        add("v", lambda q: q.tensor_tensor(o[0], a[0], b[0], op), vtime(o, [a, b], 1 if a[5] or b[5] else 2), 0, [o], [a, b])
 
     def ts(o, a, s1, op0, s2=None, op1=None):
         if s2 is None:
-            add("v", lambda q: q.tensor_scalar(o[0], a[0], P(s1), None, op0), [o], [a, s1])
+            add("v", lambda q: q.tensor_scalar(o[0], a[0], P(s1), None, op0), vtime(o, [a]), 0, [o], [a, s1])
         else:
-            add("v", lambda q: q.tensor_scalar(o[0], a[0], P(s1), P(s2), op0, op1), [o], [a, s1, s2])
+            add("v", lambda q: q.tensor_scalar(o[0], a[0], P(s1), P(s2), op0, op1), vtime(o, [a]), 0, [o], [a, s1, s2])
 
     def scan(o, a, b, init, op0, op1):
-        add("v", lambda q: q.tensor_tensor_scan(o[0], a[0], b[0], P(init), op0, op1), [o], [a, b, init])
+        add("v", lambda q: q.tensor_tensor_scan(o[0], a[0], b[0], P(init), op0, op1), vtime(o, [a, b]), 0, [o], [a, b, init])
 
     def act(o, a, fn, bias=None, scale=None, acc=None):
         kw = {}
         if bias is not None:
             kw["bias"] = P(bias)
         if scale is not None:
-            kw["scale"] = scale
+            kw["scale"] = P(scale)
         if acc is not None:
             kw["accum_out"] = acc[0]
-        add("s", lambda q: q.activation(o[0], a[0], fn, **kw), [o] + ([acc] if acc else []), [a, bias])
+        add("s", lambda q: q.activation(o[0], a[0], fn, **kw), 65 + CY * a[3] * GA if a[2] else SCALL + CY * a[3], 0,
+            [o] + ([acc] if acc else []), [a, bias, scale])
 
     def mm(o, l, r, start, stop):
-        add("t", lambda q: q.matmul(o[0], l[0], r[0], start, stop), [o], [l, r])
+        add("t", lambda q: q.matmul(o[0], l[0], r[0], start, stop), PE * max(64, r[3]) * (4 if r[4] == 4 else 1), 0, [o], [l, r])
 
     def iota(o, pattern, base, cm, whole=False):
-        if whole:
-            add("g", lambda q: q.iota(o[0], pattern, base, cm), [o], [])
-        else:
-            add("g", lambda q: q.iota(o[0], pattern, base, cm, allow_small_or_imprecise_dtypes=True), [o], [])
+        kw = {} if whole else {"allow_small_or_imprecise_dtypes": True}
+        add("g", lambda q: q.iota(o[0], pattern, base, cm, **kw), 130 + 2 * CY * o[3], 0, [o], [], behind=sends[-1:])
+
+    def zero(o):
+        iota(o, [[0, o[3]]], 0, 0)
 
     def dma(e, o, a, sem):
-        add(e, lambda q: q.dma_start(o[0], a[0]).then_inc(T.sem[sem], 16), [o], [a], sem=(sem, 16))
+        add(e, lambda q: q.dma_start(o[0], a[0]).then_inc(T.sem[sem], 16), 50, 2200, [o], [a], sem=(sem, 16))
 
-    def hbm(name):
-        return (T[name][:], [(name, 0, 1, 1)], [])
+    def hbm(name, a=None, b=None):
+        return (T[name][:] if a is None else T[name][:, a:b], [(name, 0, 1, 1)], [])
 
     others = [q for q in range(N) if q != me]
     near = [q for q in others if T.cores[q] in topo.cores_of(core)]
@@ -210,363 +344,435 @@ def rank_program(g, core, T, topo):
     def bits(es):
         return sum(1 << e for e in es)
 
-    def slot(owner, src):
-        fs = [q for q in range(N) if T.cores[q] not in topo.cores_of(T.cores[owner])]
-        return fs.index(src) if src in fs else len(fs)
+    def XIN(t, owner, src, a, b):
+        o = (3 * (t % 2) + (src - owner - 1) % N) * V
+        return A("xin", o + a, o + b)
 
-    def send(items, sem, after=()):
+    def send(items, sem, after=(), lane="d"):
         trs = []
         for q, src, dst, es, rs in items:
-            rid, pid = topo.addr(T.cores[q], core)
+            rid, pid = topo.addr(T.cores[q] if q >= 0 else _helper(me, T, topo), core)
             trs.append(RemoteDMATransfer(dst_ids=[DstId(rid=rid, pnc=pid)], dma_engine_mask=bits(es),
                                          remote_sem=T.sem[rs], src=src[0], dst=dst))
-        add("g", lambda q: q.remote_dma_fused(trs, local_sem=T.sem[sem]), [], [it[1] for it in items],
-            sem=(sem, sum(len(it[3]) for it in items)), after=after)
+        add("g", lambda q: q.remote_dma_fused(trs, local_sem=T.sem[sem]), 150, HOP + (0 if sends else FIRST),
+            [], [it[1] for it in items], sem=(sem, sum(len(it[3]) for it in items)), after=after, behind=sends[-1:])
+        sends.append(len(ops) - 1)
+        row = items[0][1][3] * items[0][1][4]
+        if lane == "n":
+            add(lane, None, 64 / h * (ROW + row / RATE) + FIRST / 2, 0, [], [], behind=sends[-1:])
+        elif lane == "r":
+            add("d", None, max(64 / h * (ROW + row / RATE), 128 * row / PORT), 0, [], [], behind=sends[-1:] + moves[-1:])
+        else:
+            add(lane, None, max(128 / h * (ROW + row / RATE), 256 * row / PORT), 0, [], [], behind=sends[-1:] + moves[-1:])
+        moves.append(len(ops) - 1)
 
     def arrive(outs, sem, n):
-        add(None, None, outs, [], sem=(sem, n))
+        add(None, None, 0, 200, outs, [], sem=(sem, n), behind=moves[-1:])
 
     h = len(efar) // 2
     eng = {far[0]: efar[:h], far[1]: efar[h:], near[0]: enear}
 
-    def send_narrow(t, ranks, a, b, tag):
-        xin = "xin%d" % t
-        send([(q, A("xu", a, b), A(xin, slot(q, me) * V + a, slot(q, me) * V + b)[0], eng[q], "a%s%d_%d" % (tag, t, me)) for q in ranks],
-             "s%s%d" % (tag, t))
+    def TAB(t, a=0, b=3080):
+        return A("tab%d" % (t % 2), a, b)
+
+    def x(t, a, b):
+        return TAB(t, me * V + a, me * V + b)
+
+    def send_narrow(a, b, c):
+        send([(q, A("xu", a, b), XIN(0, q, me, a, b)[0], eng[q], "ax0_%d_%d" % (c, me)) for q in far], "sx0_%d" % c)
+        for q in far:
+            arrive([XIN(0, me, q, a, b)], "ax0_%d_%d" % (c, q), len(eng[q]))
+
+    def send_new(t, a, b, c):
+        if WIDE[c]:
+            send([(near[0], x(t, a, b), x(t, a, b)[0], enear, "ax%d_%d_%d" % (t, c, me)),
+                  (-1, x(t, a, b), x(t, a, b)[0], efar, "ah%d" % t)], "sx%d_%d" % (t, c), lane="r")
+            arrive([TAB(t, near[0] * V + a, near[0] * V + b)], "ax%d_%d_%d" % (t, c, near[0]), len(enear))
+            for q in far:
+                arrive([TAB(t, q * V + a, q * V + b)], "ax%d_%d_%d" % (t, c, q), 8)
+                ops[-1]["hold"] = HOP + 16 * (ROW + 4 * (b - a) / RATE) + 500 + (FIRST if t == 1 else 0)
+            return
+        q, m, sem = near[0], (a + b) // 2, "ax%d_%d_%d" % (t, c, me)
+        send([(q, A("xu", a, b), XIN(t, q, me, a, b)[0], eng[q], sem) for q in far]
+             + [(q, x(t, a, m), x(t, a, m)[0], enear[:h], sem), (q, x(t, m, b), x(t, m, b)[0], enear[h:], sem)], "sx%d_%d" % (t, c))
+        arrive([TAB(t, q * V + a, q * V + b)], "ax%d_%d_%d" % (t, c, q), len(enear))
+        for q in far:
+            arrive([XIN(t, me, q, a, b)], "ax%d_%d_%d" % (t, c, q), len(eng[q]))
+        widen(t, far, a, b)
+
+    def widen(t, ranks, a, b):
         for q in ranks:
-            arrive([A(xin, slot(me, q) * V + a, slot(me, q) * V + b)], "a%s%d_%d" % (tag, t, q), len(eng[q]))
+            cp(TAB(t, q * V + a, q * V + b), XIN(t, me, q, a, b))
 
-    def send_wide(t):
-        tab, q = "tab%d" % t, near[0]
-        part = A(tab, me * V, (me + 1) * V)
-        send([(q, part, part[0], eng[q], "ax%d_%d" % (t, me))], "sz%d" % t)
-        arrive([A(tab, q * V, (q + 1) * V)], "ax%d_%d" % (t, q), len(eng[q]))
+    def F(t, a=0, b=DQ + 256, step=1):
+        return A("F", 4 * EARLY * (1 - t) + a, 4 * EARLY * (1 - t) + b, step)
 
-    def widen_x(t, ranks, a, b):
-        for q in ranks:
-            cp(A("tab%d" % t, q * V + a, q * V + b), A("xin%d" % t, slot(me, q) * V + a, slot(me, q) * V + b))
-
-    rcol, rm1, fix, nfix = A("col", 0, 1), A("col", 1, 2), A("col", 2, 3), A("col", 3, 4)
-    b0, b1, fx2, r0 = A("col", 4, 5), A("col", 5, 6), A("col", 6, 7), A("col", 7, 8)
-    TM = A("psG", 256, 512)
+    rcol, rm1, fix, nfix, b0, b1, fx2, r0, cls, clb, r1, c4, cw, pm, pa, px, py = [A("col", j, j + 1) for j in range(17)]
+    dl, dl2, dlq = A("dl", 0, 16), A("dl", 16, 32), A("dl", 32, 48)
+    ka, kb, kc, kd, ke, kf, kg = [A("k", 16 * j, 16 * j + 16) for j in range(7)]
+    kh, ki, kj, kk, kl = [A("k", 16 * j, 16 * j + 16) for j in range(11, 16)]
     pat = A("pat", 0, 256)
 
-    HV = V // 2
-    dma("y", A("xi", 0, HV), (T["x0"][:, 0:HV], [], []), "ld0")
-    dma("y", A("xi", HV, V), (T["x0"][:, HV:V], [], []), "ld5")
+    I1, I2 = A("z2", 0, 128), A("z2", 128, 256)
+    for c, (a, b) in enumerate(OPENING):
+        dma("y", A("xi", a, b), hbm("x0", a, b), "lx%d" % c)
     dma("y", A("li"), hbm("l0"), "ld1")
     dma("y", A("eai", 0, 6), hbm("ea"), "ld2")
     dma("y", A("ebi", 0, 6), hbm("eb"), "ld3")
     dma("y", A("ui", 0, 3), hbm("u"), "ld4")
-    iota(A("I2"), [[16, 8], [0, 16]], 0, -1)
-    iota(A("I1"), [[1, 128]], 0, -1)
+    iota(I2, [[16, 8], [0, 16]], 0, -1)
+    iota(I1, [[1, 128]], 0, -1)
     iota(A("pi", 0, 1), [[0, 1]], 0, 1, True)
-    iota(A("J16"), [[0, 16], [1, 16]], 0, 0)
-    iota(A("dl"), [[16, 16]], 0, 0)
-    for t in range(RO):
-        ms(A("tab%d" % t, NONE, 3080), 0.0)
-    ms(A("ones"), 1.0)
-    ms(A("ripe", V, 800), 1.0)
-    ts(A("tmpa", 0, 128), A("I2"), -15.0, OP.max, 0.0, OP.min)
-    ms(A("Lf", V, PL), float(NONE))
-    tt(A("OBf"), A("tmpa", 0, 128), A("I2"), OP.is_equal)
-    ts(A("If"), A("I1"), 0.0, OP.is_equal)
+    iota(A("mm"), [[0, 16], [1, 16]], 0, 0)
+    iota(kd, [[16, 16]], 0, 0)
+    for c, (a, b) in enumerate(OPENING):
+        cp(A("xu", a, b), A("xi", a, b))
+        send_narrow(a, b, c)
+    cp(x(0, 0, V), A("xi"))
+    send([(near[0], x(0, 0, V), x(0, 0, V)[0], enear, "an")], "sn", lane="n")
+    arrive([TAB(0, near[0] * V, near[0] * V + V)], "an", len(enear))
+    for t in range(2):
+        ms(TAB(t, NONE, 3080), 0.0)
+
+    def fill(o, c):
+        act(o, A("mm", 0, o[3]), AF.Identity, bias=c, scale=0.0)
+
+    ms(A("out0"), 0.0)
+    act(A("out1"), A("out0"), AF.Copy)
+    fill(A("nil"), 0.0)
+    fill(A("ones"), 1.0)
+    fill(A("c25"), 2.5 / 16)
+    act(A("Lf", SP, PL), A("out0", 0, PL - SP), AF.Copy)
+    fill(A("rp5"), 0.0)
+    fill(A("Mx", 384, 512), 0.0)
+    fill(A("kill", 0, 24), -float(2 ** 20))
+    fill(A("kill", 24, 32), 0.0)
+    fill(A("ripe", V, 800), 2.0)
+    ts(A("PA", 0, 128), I2, -15.0, OP.max, 0.0, OP.min)
+    fill(A("Lf", V, SP), float(NONE))
+    tt(A("OBf"), A("PA", 0, 128), I2, OP.is_equal)
+    ts(A("If"), I1, 0.0, OP.is_equal)
     ts(A("pa", 0, 1), A("pi", 0, 1), 15, OP.bitwise_and)
-    ts(A("tmpa", 128, 256), A("I1"), 0.0, OP.is_gt)
-    ts(A("tmpa", 256, 384), A("I1"), 0.0, OP.is_lt, -1.0, OP.mult)
+    ts(A("PA", 128, 256), I1, 0.0, OP.is_gt)
+    ts(A("PA", 256, 384), I1, 0.0, OP.is_lt, -1.0, OP.mult)
     cp(rcol, A("pa", 0, 1))
     act(A("OB"), A("OBf"), AF.Copy)
-    act(A("tmpb", 128, 256), A("If"), AF.Copy, scale=-128.0)
+    act(A("PB", 128, 256), A("If"), AF.Copy, scale=-128.0)
     act(A("z", 0, 128), A("If"), AF.Copy, scale=-4096.0)
-    act(A("NIf"), A("If"), AF.Copy, scale=-1.0)
+    act(A("Hf"), A("If"), AF.Copy, scale=0.5)
+    act(A("NOH"), A("OBf"), AF.Copy, scale=-0.5)
     act(A("NOB"), A("OBf"), AF.Copy, scale=-1.0)
-    act(A("OB20"), A("OBf"), AF.Copy, scale=-20.0)
-    act(A("OB125"), A("OBf"), AF.Copy, scale=1.25)
-    tt(A("tmpb", 0, 128), A("tmpa", 128, 256), A("OBf"), OP.mult)
-    tt(A("tmpb", 256, 384), A("tmpa", 256, 384), A("OBf"), OP.mult)
-    cp(A("xu", 0, HV), A("xi", 0, HV))
-    send_narrow(0, others, 0, HV, "x")
-    cp(A("xu", HV, V), A("xi", HV, V))
-    send_narrow(0, others, HV, V, "y")
-    iota(A("lift", 0, NV), [[0, NV // 32], [4096, 32]], 0, 0)
+    tt(A("PB", 0, 128), A("PA", 128, 256), A("OBf"), OP.mult)
+    tt(A("PB", 256, 384), A("PA", 256, 384), A("OBf"), OP.mult)
+    iota(A("lift"), [[0, 8], [4096, 32]], 0, 0)
     iota(A("G", 0, 512), [[4096, 32], [0, 16]], 0, 0)
+    act(A("liftG"), A("G", 0, 512), AF.Copy, scale=16.0)
+    iota(A("T3", 0, V), [[0, 3], [4096, 256]], 0, 0)
+    fill(A("T3", V, WN), 0.0)
     iota(A("T1"), [[1, 3104]], 0, 0)
-    iota(A("T2", 0, NONE), [[0, N], [4096, V]], 0, 0)
-    for k in range(4):
-        act(A("RP", 256 * k, 256 * k + 256), A("J16"), AF.Sign)
-    cp(A("tab0", me * V, (me + 1) * V), A("xi"))
-    tt(A("TriEr"), A("tmpb", 0, 128), A("tmpb", 128, 256), OP.add)
-    tt(A("NTriU"), A("tmpb", 256, 384), A("z", 0, 128), OP.add)
+    zero(A("accW"))
+    zero(A("D0", 0, DUM))
+    for k in range(0, FOLD, 256):
+        act(A("RP", k, k + 256), A("mm"), AF.Sign)
+    fill(A("ramp", 1, 512, 2), 0.0)
+    act(A("ramp", 0, 512, 2), A("T3", 0, 256), AF.Copy)
+    tt(A("TriEr"), A("PB", 0, 128), A("PB", 128, 256), OP.add)
+    tt(A("NTriU"), A("PB", 256, 384), A("z", 0, 128), OP.add)
     ts(r0, rcol, 0.0, OP.is_equal)
-    ts(b0, rcol, -1.0, OP.mult, -0.5, OP.add)
-    ts(b1, rcol, -1.0, OP.mult, -16.5, OP.add)
-    ts(A("t0", 0, 16), A("J16", 0, 16), rcol, OP.is_gt)
+    ts(b0, rcol, -2.0, OP.mult, -1.0, OP.add)
+    ts(b1, rcol, -2.0, OP.mult, -33.0, OP.add)
+    ts(A("TM"), A("mm"), rcol, OP.is_gt)
     ts(rm1, r0, 16.0, OP.mult, rcol, OP.add)
     ts(fix, r0, -2 * BIG, OP.mult, BIG, OP.add)
-    ts(A("y2", 0, 16), A("J16", 0, 16), rcol, OP.is_equal, -BIG, OP.mult)
-    ts(A("dl2"), A("dl"), rcol, OP.add, 800.0, OP.add)
+    ts(A("t0", 0, 128), A("mm", 0, 128), rcol, OP.is_equal, -BIG, OP.mult)
+    ts(dl2, kd, rcol, OP.add, float(WN), OP.add)
     ts(rm1, rm1, -1.0, OP.add)
     ts(nfix, fix, -1.0, OP.mult)
     ts(fx2, fix, 1.0 / 4096, OP.mult, -0.375, OP.add)
-    ts(A("kd"), A("dl2"), float(DUM - 800), OP.add)
-    ts(A("zz", 0, 16), A("J16", 0, 16), rm1, OP.is_equal, 2 * BIG, OP.mult)
-    ms(A("c25"), 2.5 / 16)
-    tt(A("pat", 0, 16), A("y2", 0, 16), A("zz", 0, 16), OP.add)
-    for n in (16, 32, 64, 128):
-        act(A("pat", n, 2 * n), A("pat", 0, n), AF.Copy)
-        act(A("t0", n, 2 * n), A("t0", 0, n), AF.Copy)
-    act(A("pat", 256, 384), A("pat", 0, 128), AF.Copy)
-    act(TM, A("t0"), AF.Copy)
-    act(A("liftG"), A("G", 0, 512), AF.Copy, scale=16.0)
-    for k in range(0, 5 * RQ, 1024):
-        n = min(1024, 5 * RQ - k)
-        act(A("accW", k, k + n), A("RP", 0, n), AF.Copy, scale=0.0)
-    cp(A("L16"), A("li"))
-    ms(A("lift", NV, 256), 0.0)
+    ts(dl, dl2, float(DUM - WN), OP.add)
+    ts(dlq, dl2, float(DQ - WN), OP.add)
+    ts(A("t0", 128, 256), A("mm", 0, 128), rm1, OP.is_equal, 2 * BIG, OP.mult)
+    ts(cls, r0, -2.0, OP.mult, 1.0, OP.add)
+    ts(clb, r0, 19.0, OP.mult, -15.0, OP.add)
+    ts(r1, rcol, 1.0, OP.is_equal, -40.0, OP.mult)
+    ts(c4, nfix, 2.5, OP.add)
+    ts(cw, nfix, float(NONE), OP.add)
+    ts(pm, rcol, 8.0, OP.is_lt, 4.0, OP.mult)
+    ts(pa, rcol, float(DQ), OP.add)
+    ts(px, rcol, 8.0, OP.is_ge)
+    ts(r1, r0, 40.0, OP.mult, r1, OP.add)
+    ts(pa, pa, px, OP.mult)
+    tt(A("pat", 0, 128), A("t0", 0, 128), A("t0", 128, 256), OP.add)
+    act(A("OB40"), A("OBf"), AF.Copy, scale=r1)
+    for n in (128, 256):
+        act(A("pat", n, n + 128), A("pat", 0, 128), AF.Copy)
     cp(A("Lf", 0, V), A("li"))
-    ms(A("rp5"), 0.0)
-    for d in range(5):
-        ms(A("c26", d, 130, 5), (RQ * d + 4096) / 16.0)
-    ts(A("rp5", 0, 130, 5), A("rp5", 0, 130, 5), 16384.0, OP.add)
-    cp(A("dl"), A("kd"))
-    ms(A("T2", NONE, 3080), 0.0)
-    ms(A("erT", V, 776), 0.0)
-    ms(A("wT", V, 776), 2.5)
-    ms(A("clr", 24, 32), 0.0)
+    fill(A("r26"), 1.0)
+    iota(A("c26"), [[0, 26], [RQ // 16, 5]], 256, 0)
+    fill(A("rp5", 0, 130, 5), 16384.0)
+    fill(A("r26", 0, 130, 26), 0.0)
+    fill(A("clr", 24, 32), 0.0)
     ts(A("af", 0, 6), A("eai", 0, 6), float(me * V), OP.add)
     cp(A("bf", 0, 6), A("ebi", 0, 6))
     cp(A("eb16", 0, 6), A("ebi", 0, 6))
     ts(A("uc", 0, 3), A("ui", 0, 3), -0.25, OP.add)
     cp(A("ea16", 0, 6), A("af", 0, 6))
     tt(A("amb", 0, 6), A("af", 0, 6), A("bf", 0, 6), OP.subtract)
-    ts(A("em"), A("L16"), float(NONE), OP.is_equal)
-    widen_x(0, near + far, 0, HV)
-    widen_x(0, near + far, HV, V)
+    for a, b in OPENING:
+        widen(0, far, a, b)
 
-    for t in range(RO):
-        tab = A("tab%d" % t)
-        last = t == RO - 1
+    ring = [0]
+
+    def stage(a, lo=0, hi=None, step=1):
+        return A(("psH", "psG", "psH")[a // 256], lo, 2 * min(256, EARLY - a) if hi is None else hi, step)
+
+    def half(a, b):
+        return A("psS", a + 256, b + 256) if a < 512 else A("psD", a + 512 - LAST, b + 512 - LAST)
+
+    def half_open(t, a, b, up):
+        mm(half(a, b), A("Hf"), x(t, a, b), True, False)
+        if up:
+            mm(half(a, a + up[3]), A("NOH"), up, False, False)
+
+    def gather(t, a, b):
+        joins = t and a < EARLY
+        if joins:
+            mm(stage(a), A("OB"), A("ramp", 0, 2 * (b - a)), True, False)
+            mm(stage(a, 0, 2 * (b - a), 2), A("OB"), A("out%d" % (t - 1), a, b), False, False)
+            if a == 512:
+                second(t, a, b)
+        mine = OWN if a == t == 0 else 0
+        if not joins:
+            half_open(t, a, b, A("lift", 0, mine) if mine else None)
+        n = 64 if a < LAST else 32
+        for v in range(a, b, n):
+            go, mo = 1024 * (ring[0] % GS), 1024 * (ring[0] % 4)
+            ring[0] += 1
+            if v < a + mine:
+                for k in (0, 512):
+                    tt(A("G", go + k, go + k + 512), X(TAB(t), A("L16", v + k // 16, v + k // 16 + 32)), A("liftG"), OP.add)
+                    scan(A("MS", mo + k + 1, mo + k + 512, 2), A("G", go + k, go + k + 512, 2), A("G", go + k + 1, go + k + 512, 2),
+                         0.0, OP.max, OP.max)
+            else:
+                act(A("G", go, go + 16 * n), X(TAB(t), A("L16", v, v + n)), AF.Copy)
+                w = min(FOLD, 16 * n)
+                for k in range(0, 16 * n, w):
+                    scan(A("MS", mo + k, mo + k + w), A("RP", 0, w), A("G", go + k, go + k + w), 0.0, OP.mult, OP.max)
+            Mv = A("MS", mo + 15, mo + 16 * n, 16)
+            if joins:
+                mm(stage(a, 2 * (v - a), 2 * (v - a + n), 2), A("If"), Mv, False, v + n == LAST)
+            else:
+                mm(half(v, v + n), A("Hf"), Mv, False, v + n == b)
+
+    def second(t, a, b):
+        mm(stage(a, 1, 2 * (b - a), 2), A("If"), F(t - 1, 4 * a + 1, 4 * b, 4), False, a < 512)
+
+    def join(t, a, b):
+        scan(A("Q", 2 * a, 2 * b), stage(a), F(t - 1, 4 * a, 4 * b, 2), 0.0, OP.max, OP.max)
+        half_open(t, a, b, A("ramp", 0, 2 * (b - a), 2))
+        mm(half(a, b), A("Hf"), A("Q", 2 * a + 1, 2 * b, 2), False, True)
+
+    def degrees():
+        act(A("em", 0, V), A("Lf", 0, V), AF.Relu, bias=1.0 - NONE)
+        for a, b in ((0, 512), (512, V)):
+            mm(A("psE", a, b), A("OB"), A("em", a, b), True, True)
+        act(A("cl"), A("psE", 0, V), AF.Relu, bias=clb, scale=cls)
+
+    def choose(t, k):
+        a, b = BLOCKS[k]
+        mm(A("psE", a, b), A("OB40"), A("cl", a, b), True, False)
+        tt(A("gt", a, b), half(a, b), x(t, a, b), OP.is_lt)
+        mm(A("psE", a, b), A("OB"), A("gt", a, b), False, True)
+        bar = 11.5
+        if RIPE[t][k] == "s":
+            act(A("ripe", a, b), A("psE", a, b), AF.Sign, bias=-bar)
+        else:
+            ts(A("ripe", a, b), A("psE", a, b), bar, OP.is_gt, 2.0, OP.mult)
+        e = 800 if b == V else b
+        scan(A("cum", a, e), A("ones" if RIPE[t][k] == "s" else "nil", 0, e - a), A("ripe", a, e),
+             A("cum", a - 1, a) if a else 0.0, OP.add, OP.add)
+
+    def places(k, a, b):
+        act(A("em", a, b), A("cum", a, b), AF.Sign, bias=b0, acc=A("cnt", 2 * k, 2 * k + 1))
+        act(A("gt", a, b), A("cum", a, b), AF.Sign, bias=b1, acc=A("cnt", 2 * k + 1, 2 * k + 2))
+
+    def new_x(t, c):
+        a, b = PIECES[c]
+        ts(A("xu", a, b), half(a, b), A("uc", t, t + 1), OP.add)
+        if t == RO - 1:
+            cp(A("Q", a, b), A("xu", a, b))
+        else:
+            cp(x(t + 1, a, b), A("xu", a, b))
+            send_new(t + 1, a, b, c)
+
+    def edges(t):
         e2 = (2 * t, 2 * t + 2)
-
-        def x(a, b):
-            return A("tab%d" % t, me * V + a, me * V + b)
-
-        def gslot(c):
-            return A("G", 1024 * (c % 6), 1024 * (c % 6) + 16 * (SCH[c][1] - SCH[c][0]))
-
-        def gather(c):
-            act(gslot(c), X(tab, A("L16", *SCH[c])), AF.Copy)
-
-        def fold(c):
-            a, b = SCH[c]
-            scan(A("MS", 16 * (a % 512), 16 * (a % 512 + b - a)), A("RP", 0, 16 * (b - a)), gslot(c), 0.0, OP.mult, OP.max)
-            if c + 6 < len(SCH):
-                gather(c + 6)
-
-        def own_gather(k):
-            tt(A("Gv", 512 * (k % 2), 512 * (k % 2) + 512), X(tab, A("L16", 32 * k, 32 * k + 32)), A("liftG"), OP.add)
-
-        def own_fold(k):
-            o = 512 * (k % 2)
-            scan(A("MS", 512 * k + 1, 512 * k + 512, 2), A("Gv", o, o + 512, 2), A("Gv", o + 1, o + 512, 2), 0.0, OP.max, OP.max)
-
-        def M(a, b):
-            return A("MS", 16 * (a % 512) + 15, 16 * (a % 512 + b - a), 16)
-
-        def diff_open(a, b):
-            mm(A("psD", a, b), A("If"), x(a, b), True, False)
-            if a == 0:
-                mm(A("psD", a, b), A("OB"), A("lift", a, b), False, False)
-
-        def diff_close(a, b):
-            mm(A("psD", a, b), A("NIf"), M(a, b), False, True)
-
-        def score_open(a, b):
-            mm(A("psE", a, b), A("OB20"), A("em", a, b), True, False)
-            mm(A("psE", a, b), A("OB125"), A("cl", a, b), False, False)
-
-        def total_open():
-            mm(A("psS", 0, 512), A("If"), x(0, 512), True, False)
-            mm(A("psS", 0, 256), A("NOB"), A("lift"), False, False)
-            mm(A("psS", 512, V), A("If"), x(512, V), True, False)
-
-        def total(a, b):
-            mm(A("psS", a, b), A("If"), M(a, b), False, a > 0)
-
-        def votes(a, b):
-            ts(A("gt", a, b), A("psD", a, b), 0.5, OP.is_gt)
-            mm(A("psE", a, b), A("OB"), A("gt", a, b), False, True)
-
-        def ripe(a, b):
-            ts(A("ripe", a, b), A("psE", a, b), 12.0, OP.is_ge)
-
-        def count(a, b):
-            scan(A("cum", a, b), A("ones", 0, b - a), A("ripe", a, b), A("cum", a - 1, a) if a else 0.0, OP.mult, OP.add)
-
-        def new_x(a, b):
-            ts(A("xu", a, b), A("psS", a, b), 0.5, OP.mult, A("uc", t, t + 1), OP.add)
-
-        def empties(ps, l):
-            mm(A(ps, 0, 512), A(l), A("em", 0, 512), True, True)
-            mm(A(ps, 512, V), A(l), A("em", 512, V), True, True)
-
-        iota(A("D", 0, 2 * PL + 776), [[0, 2 * PL + 776]], 0, 0)
-        diff_open(0, 256)
-        diff_open(512, 640)
-        total_open()
-        for c in range(6):
-            gather(c)
-        own_gather(0)
-        if t:
-            ts(A("em"), A("L16"), float(NONE), OP.is_equal)
-        empties("psE", "OB")
-        own_fold(0)
-        fold(0)
-        cp(A("xa"), X(tab, A("ea16", *e2)))
-        ts(A("cl"), A("psE", 0, V), 4.0, OP.max, 15.0, OP.min)
-        tt(A("dd"), X(tab, A("eb16", *e2)), A("xa"), OP.subtract)
+        act(A("xa"), X(TAB(t), A("ea16", *e2)), AF.Copy)
+        tt(A("dd"), X(TAB(t), A("eb16", *e2)), A("xa"), OP.subtract)
         mm(A("psG", 160, 192), A("OBf"), A("dd"), True, True)
-        score_open(0, 256)
-        score_open(512, 640)
-        fold(1)
-        own_gather(1)
         scan(A("ez"), A("psG", 160, 192), A("pat", 0, 32), nfix, OP.min, OP.add)
-        own_fold(1)
         ts(A("ef"), A("ez", 15, 32, 16), fix, OP.add, 0.0, OP.is_ge)
-        fold(2)
         tt(A("et"), A("ef"), A("amb", *e2), OP.mult)
-        own_gather(2)
         tt(A("RL", 0, 2), A("et"), A("bf", *e2), OP.add)
         tt(A("gv"), A("af", *e2), A("et"), OP.subtract)
-        own_fold(2)
-        diff_close(0, 256)
-        fold(3)
         cp(A("giv16", 0, 2), A("gv"))
-        votes(0, 256)
-        total(0, 256)
-        diff_open(256, 512)
-        fold(4)
-        ripe(0, 256)
-        score_open(256, 512)
-        for d in range(4):
-            ms(A("SW", RQ * d, RQ * d + 64), 4096.0 * V)
-        count(0, 256)
-        fold(5)
-        fold(6)
-        diff_close(256, 512)
-        fold(7)
-        votes(256, 512)
-        total(256, 512)
-        fold(8)
-        diff_close(512, 640)
-        ripe(256, 512)
-        if not last:
-            new_x(0, CUT)
-            send_narrow(t + 1, far, 0, CUT, "x")
-        count(256, 512)
-        votes(512, 640)
-        fold(9)
-        ripe(512, 640)
-        score_open(640, V)
-        count(512, 640)
-        fold(10)
-        act(A("junk", 0, 640), A("cum", 0, 640), AF.Sign, bias=b0, acc=A("cnt", 0, 1))
-        act(A("junk", 640, 1280), A("cum", 0, 640), AF.Sign, bias=b1, acc=A("cnt", 1, 2))
-        fold(11)
-        tt(A("gt", 640, V), x(640, V), M(640, V), OP.is_gt)
-        mm(A("psE", 640, V), A("OB"), A("gt", 640, V), False, True)
-        ripe(640, V)
-        count(640, 800)
-        act(A("junk", 0, 160), A("cum", 640, 800), AF.Sign, bias=b0, acc=A("cnt", 2, 3))
-        act(A("junk", 160, 320), A("cum", 640, 800), AF.Sign, bias=b1, acc=A("cnt", 3, 4))
-        ts(A("cs"), A("cnt", 0, 2), -0.5, OP.mult, 400.0, OP.add)
-        for c in range(2):
-            ts(A("vs16", c, c + 1), A("cnt", 2 + c, 3 + c), -0.5, OP.mult, A("cs", c, c + 1), OP.add)
 
+    def free_slots():
+        for d in range(4):
+            iota(A("SW", RQ * d, RQ * d + 64), [[0, 64]], 4096 * SP, 0)
+
+    def values(t):
+        for k, (a, b) in enumerate(BLOCKS):
+            if t == 0 or a >= 512:
+                gather(t, a, b)
+            if t and a < EARLY:
+                join(t, a, b)
+            choose(t, k)
+            for c, piece in enumerate(PIECES):
+                if b == piece[1]:
+                    new_x(t, c)
+            if k:
+                places(k - 1, 0 if k == 1 else a, 800 if b == V else b)
+        tt(A("cs"), A("cnt", 0, 2), A("cnt", 2, 4), OP.add)
+        ts(A("cs"), A("cs"), -0.5, OP.mult, 400.0, OP.add)
+        for c in range(2):
+            ts(A("vs16", c, c + 1), A("cnt", 4 + c, 5 + c), -0.5, OP.mult, A("cs", c, c + 1), OP.add)
+
+    def requests(t):
         mm(A("psG", 0, 130), A("OB"), A("c26"), True, False)
         cp(A("RL", 2, 34), X(A("Lf", 0, 800), A("vs16")))
         cp(A("vsb"), X(A("T1", me * V, me * V + 800), A("vs16")))
         ts(A("o16"), A("RL", 0, 26), 1.0 / V, OP.mult, -0.4995, OP.add)
-        cp(A("R16"), A("RL", 0, 26))
         cp(A("giv16", 2, 26), A("vsb", 0, 24))
-        act(A("PA"), X(A("T2"), A("R16")), AF.Copy)
         act(A("PB"), X(A("T1"), A("giv16")), AF.Identity, bias=float(NONE), scale=-1.0)
+        ts(A("k", 112, 138), A("o16"), -float(V), OP.mult)
+        tt(A("k", 144, 170), A("k", 112, 138), A("RL", 0, 26), OP.add)
+        cp(A("R16"), A("k", 144, 170))
+        act(A("PA"), X(A("T1", 0, V), A("R16")), AF.Copy, scale=4096.0)
         for d in range(5):
-            ts(A("own", d, 130, 5), A("o16"), float(d), OP.is_equal)
-        mm(A("psG", 0, 130), A("NTriU"), A("own"), False, False)
+            ts(A("own", 26 * d, 26 * d + 26), A("o16"), float(d), OP.is_equal)
+            mm(A("psG", d, 130, 5), A("NTriU"), A("own", 26 * d, 26 * d + 26), False, False)
+        scan(A("osc"), A("r26"), A("own"), 0.0, OP.mult, OP.add)
         for d in range(5):
-            scan(A("osc", d, 130, 5), A("ones", 0, 26), A("own", d, 130, 5), 0.0, OP.mult, OP.add)
-        mm(A("psG", 0, 130), A("OB"), A("osc"), False, True)
-        total(512, V)
-        empties("psE", "OB")
-        empties("psD", "TriEr")
+            mm(A("psG", d, 130, 5), A("OB"), A("osc", 26 * d, 26 * d + 26), False, d == 4)
         scan(A("oy"), A("rp5"), A("psG", 0, 130), 0.0, OP.add, OP.min)
         ts(A("off16"), A("oy", 4, 130, 5), -1.0, OP.add)
         tt(X(A("SW"), A("off16")), A("PA"), A("PB"), OP.add)
-        Pw = "Pw%d" % t
+        Pw = "Pw%d" % (t % 2)
         send([(q, A("SW", RQ * q, RQ * q + 64), A(Pw, 64 * me, 64 * me + 64)[0], eng[q], "ap%d" % t) for q in others],
              "sp%d" % t, after=[A("accW")])
         arrive([A(Pw, 64 * q, 64 * q + 64) for q in others], "ap%d" % t, 2 * h + len(enear))
-        act(A("wT", 0, V), A("psE", 0, V), AF.Relu, bias=2.5, scale=-1.0)
-        act(A("erT", 0, V), A("psD", 0, V), AF.Relu, bias=-125.5, scale=-1.0)
-        new_x(0 if last else CUT, V)
-        cp(A(Pw, 64 * me, 64 * me + 64), A("SW", RQ * me, RQ * me + 64))
-        if last:
-            cp(A("xo"), A("xu"))
-            dma("y", hbm("yx"), A("xo"), "st0")
-        else:
-            send_narrow(t + 1, far, CUT, V, "y")
-            cp(A("tab%d" % (t + 1), me * V, (me + 1) * V), A("xu"))
-            send_wide(t + 1)
-            widen_x(t + 1, far, 0, CUT)
+        act(A(Pw, 64 * me, 64 * me + 64), A("SW", RQ * me, RQ * me + 64), AF.Copy)
 
+    def verdicts(t):
+        Pw = A("Pw%d" % (t % 2))
         mm(A("psH", 0, 256), A("OB"), A("c25"), True, False)
-        scan(A("z"), A(Pw), pat, nfix, OP.min, OP.add)
-        ts(A("r16"), A(Pw), 1.0 / 4096, OP.mult, -0.375, OP.add)
+        scan(A("z"), Pw, pat, nfix, OP.min, OP.add)
+        ts(A("r16"), Pw, 1.0 / 4096, OP.mult, -0.375, OP.add)
         ts(A("rl16"), A("z", 15, 256, 16), 1.0 / 4096, OP.mult, fx2, OP.add)
+        act(A("emr"), X(A("Lf", 0, WN), A("rl16")), AF.Relu, bias=1.0 - NONE)
         cp(A("rlf"), A("rl16"))
-        act(A("wg"), X(A("wT"), A("rl16")), AF.Copy)
-        act(A("erg"), X(A("erT"), A("rl16")), AF.Copy)
-        act(A("t0"), X(A("Lf", 0, 776), A("rl16")), AF.Copy)
+        mm(A("psE", 0, 256), A("OB"), A("emr"), True, True)
+        mm(A("psD", 0, 256), A("TriEr"), A("emr"), True, True)
+        act(A("wg"), A("psE", 0, 256), AF.Relu, bias=2.5, scale=-1.0)
+        act(A("erg"), A("psD", 0, 256), AF.Relu, bias=-125.5, scale=-1.0)
         for c in range(16):
-            ts(A3("E", c, c + 1, slice(0, 256 - 16 * c)), A("r16", 16 * c, 256), A("rlf", c, c + 1), OP.is_equal)
+            ts(A3("E", c, c + 1, 0, 256 - 16 * c), A("r16", 16 * c, 256), A("rlf", c, c + 1), OP.is_equal)
             if c < 15:
-                mm(A("psH", 16 * c + 16, 256), A("NOB"), A3("E", c, c + 1, slice(16, 256 - 16 * c)), False, False)
-        tt(A("Ed"), A3("E", 0, 16, slice(0, 16)), TM, OP.mult)
+                mm(A("psH", 16 * c + 16, 256), A("NOB"), A3("E", c, c + 1, 16, 256 - 16 * c), False, False)
+        tt(A("Ed"), A3("E", 0, 16, 0, 16), A("TM"), OP.mult)
         mm(A("psH", 0, 256), A("NOB"), A("Ed"), False, True)
-        tt(A("gm"), X(A("T2", 0, 776), A("rl16")), A(Pw), OP.subtract)
         tt(A("acc"), A("psH", 0, 256), A("wg"), OP.is_gt)
-        send([(q, A("acc", 64 * q, 64 * q + 64), A("accW", RQ * me, RQ * me + 64)[0], eng[q], "ar%d" % t) for q in others], "sr%d" % t)
+        send([(q, A("acc", 64 * q, 64 * q + 64), A("accW", RQ * me, RQ * me + 64)[0], eng[q], "ar%d" % t) for q in others], "sr%d" % t,
+             after=[A("xin", 3 * V * (t % 2), 3 * V * (t % 2 + 1))])
         arrive([A("accW", RQ * q, RQ * q + 64) for q in others], "ar%d" % t, 2 * h + len(enear))
         act(A("accW", RQ * me, RQ * me + 64), A("acc", 64 * me, 64 * me + 64), AF.Copy)
-
-        scan(A("z"), A("psH", 0, 256), pat, nfix, OP.min, OP.add)
-        ts(A("rl2"), A("rlf"), 2.5 * PL, OP.add)
-        ts(A("ka"), A("z", 15, 256, 16), fix, OP.add, -float(PL), OP.mult)
+        act(ke, A("rlf"), AF.Identity, bias=cw, scale=4096.0)
+        tt(kf, ke, A("z", 15, 256, 16), OP.subtract)
+        cp(A("w16"), kf)
+        act(A("gm"), X(A("T1"), A("w16")), AF.Identity, bias=-float(NONE))
+        scan(A("z2"), A("psH", 0, 256), pat, nfix, OP.min, OP.add)
         tt(A("mm"), A("psH", 0, 256), A("erg"), OP.is_equal)
-        tt(A("kb"), A("ka"), A("rl2"), OP.add)
-        tt(A("kc"), A("kb"), A("dl"), OP.min)
-        tt(A("kd"), A("kb"), A("dl2"), OP.min)
-        cp(A("od16"), A("kc"))
-        cp(A("ol16"), A("kd"))
-        tt(X(A("D"), A("od16")), A("mm"), A("gm"), OP.mult)
-        act(A("t3"), X(A("D", 2 * PL, 2 * PL + 776), A("rl16")), AF.Copy)
-        act(A("y2"), X(A("accW"), A("off16", 2, 26)), AF.Copy)
-        tt(A("t1"), X(A("D", 0, 776), A("rl16")), A("t0"), OP.add)
-        tt(A("t2"), X(A("D", PL, PL + 776), A("rl16")), A("t1"), OP.add)
-        tt(X(A("Lf"), A("ol16")), A("t2"), A("t3"), OP.add)
-        if not last:
-            widen_x(t + 1, far[:1], CUT, V)
-        cp(A("lc"), X(A("Lf", 0, 800), A("vs16")))
-        if not last:
-            widen_x(t + 1, far[1:], CUT, V)
-        scan(A("zz"), A("y2"), A("pat"), nfix, OP.min, OP.add)
-        ts(A("clr", 0, 24), A("zz", 15, 384, 16), fix, OP.add, float(NONE), OP.mult)
-        tt(X(A("Lf", 0, 800), A("vs16")), A("lc"), A("clr"), OP.max)
-        if last:
-            dma("y", hbm("yl"), A("Lf", 0, V), "st1")
+
+    def answers():
+        act(A("PA", 0, 384), X(A("accW"), A("off16", 2, 26)), AF.Copy)
+        scan(A("PB", 0, 384), A("PA", 0, 384), A("pat"), nfix, OP.min, OP.add)
+        ts(A("clr", 0, 24), A("PB", 15, 384, 16), fix, OP.add, float(NONE), OP.mult)
+
+    def lists(t):
+        D = "D%d" % (t % 2)
+        act(A("wg"), X(A("Lf", 0, WN), A("rl16")), AF.Copy)
+        act(kg, A("rlf"), AF.Identity, bias=2.5 * PL)
+        ts(ka, A("z2", 15, 256, 16), fix, OP.add, -float(PL), OP.mult)
+        tt(kb, ka, kg, OP.add)
+        tt(kc, kb, dl, OP.min)
+        tt(kd, kb, dl2, OP.min)
+        cp(A("od16"), kc)
+        cp(A("ol16"), kd)
+        tt(X(A(D), A("od16")), A("mm"), A("gm"), OP.mult)
+        act(A("erg"), X(A(D, 2 * PL, 2 * PL + WN), A("rl16")), AF.Copy)
+        tt(A("gm"), X(A(D, 0, WN), A("rl16")), A("wg"), OP.add)
+        tt(A("mm"), X(A(D, PL, PL + WN), A("rl16")), A("gm"), OP.add)
+        tt(X(A("Lf"), A("ol16")), A("mm"), A("erg"), OP.add)
+        answers()
+        cp(A("lc", 0, 32), X(A("Lf", 0, 800), A("vs16")))
+        if t == RO - 1:
+            tt(X(A("Lf", 0, 800), A("vs16")), A("lc", 0, 32), A("clr"), OP.max)
+            return
+        tt(A("lc", 32, 64), A("lc", 0, 32), A("clr"), OP.max)
+        cp(A("Lx16"), A("lc", 32, 64))
+        cp(X(A("Lf", 0, 800), A("vs16")), A("lc", 32, 64))
+        cp(A("L16", EARLY, V), A("Lf", EARLY, V))
+
+    def newcomers(t):
+        zk = A("z2", 15, 256, 16)
+        act(kh, A("rlf"), AF.Identity, bias=c4, scale=4.0)
+        ts(ki, zk, nfix, OP.is_lt, 8000.0, OP.mult)
+        tt(kj, kh, zk, OP.subtract)
+        tt(kk, kj, ki, OP.add)
+        tt(kl, kk, dlq, OP.min)
+        cp(A("of16"), kl)
+        act(A("t0"), X(A("T3"), A("rl16")), AF.Copy, scale=16.0)
+        tt(A("z"), X(TAB(t + 1), A("w16")), A("t0"), OP.add)
+        tt(X(F(t), A("of16")), A("z"), A("acc"), OP.mult)
+        second(t + 1, 0, 256)
+        second(t + 1, 256, 512)
+        ts(A("p16", 0, 1), A("vs16", 0, 1), 4.0, OP.mult)
+        ts(A("p16", 1, 2), A("vs16", 1, 2), pm, OP.mult, pa, OP.add)
+        act(A("liftx"), X(A("T3"), A("vs16")), AF.Copy, scale=16.0)
+        act(A("PA", 0, 384), X(TAB(t + 1), A("Lx16", 0, 24)), AF.Copy)
+        scan(A("Mx", 0, 384), A("RP", 0, 384), A("PA", 0, 384), 0.0, OP.mult, OP.max)
+        tt(X(F(t), A("p16", 0, 2)), A("Mx", 15, 512, 16), A("liftx"), OP.add)
+
+    cp(A("L16"), A("li"))
+    degrees()
+    edges(0)
+    for t in range(RO):
+        if t:
+            verdicts(t - 1)
+            cp(X(A("out%d" % (t - 1)), A("vs16")), A("kill"))
+            gather(t, 0, 256)
+            gather(t, 256, 512)
+            free_slots()
+            zero(A("D%d" % (t % 2), 0, DUM))
+            if t == 1:
+                zero(F(1, 0, 4 * EARLY))
+            lists(t - 1)
+            newcomers(t - 1)
+            degrees()
         else:
-            cp(A("L16", NV, 192), A("Lf", NV, 192))
-            cp(A("L16", 0, NV), A("Lf", 0, NV))
-            cp(A("L16", 192, V), A("Lf", 192, V))
+            free_slots()
+        values(t)
+        if t == 1:
+            cp(A("L16", 0, EARLY), A("Lf", 0, EARLY))
+        requests(t)
+        if t == 0:
+            zero(F(0, 0, 4 * EARLY))
+        if t < RO - 1:
+            edges(t + 1)
+
+    dma("y", hbm("yx"), A("Q", 0, V), "st0")
+    verdicts(RO - 1)
+    lists(RO - 1)
+    dma("y", hbm("yl"), A("Lf", 0, V), "st1")
     _emit(g, T, ops)

from concourse.bass import DstId, RemoteDMATransfer
from concourse.mybir import AluOpType as OP, ActivationFunctionType as AF

N, V, RO = 4, 768, 3
NONE = N * V
RQ = 416
BIG = float(2 ** 22)
SP = 800
WN = 808
PL = 1064
DUM = 2936
DQ = 4 * WN
F32, B16, I32, U16 = "float32", "bfloat16", "int32", "uint16"
EARLY = 512
LAST = 704
BLOCKS = [(0, 256), (256, 512), (512, LAST), (LAST, V)]
PIECES = [(0, 512), (512, V)]
WIDE = [True, False]
OPENING = [(0, 256), (256, V)]
OWN = 128
GS = 7
RIPE = ["sssv", "sssv", "sssv"]
CY, VC, SCALL, GA, SC, PE, SYNC, HOP, FIRST = 0.83, 55.0, 150.0, 1.75, 3.8, 0.7, 100.0, 700.0, 1800.0
FOLD = 1024
ROW, RATE, PORT = 35.0, 30.0, 100.0
TURNS = 4000
PLANS = {}


def _sb(n, d):
    return ("sbuf", [128, n], d)


SCRATCH = {
    "xi": _sb(V, I32), "li": _sb(V, I32), "eai": _sb(8, I32), "ebi": _sb(8, I32), "ui": _sb(4, I32),
    "tab0": _sb(3080, F32), "tab1": _sb(3080, F32),
    "xu": _sb(V, U16), "xin": _sb(6 * V, U16),
    "Lf": _sb(PL, F32), "L16": _sb(V, U16), "Lx16": _sb(32, U16),
    "G": _sb(1024 * GS, F32), "MS": _sb(4096, F32),
    "Q": _sb(2 * EARLY, F32), "Mx": _sb(512, F32), "RP": _sb(FOLD, B16),
    "T1": _sb(3104, F32), "T3": _sb(WN, F32),
    "D0": _sb(DQ + 256, F32), "D1": _sb(DQ + 256, F32), "F": _sb(4 * EARLY + DQ + 256, F32),
    "out0": _sb(800, B16), "out1": _sb(800, B16), "kill": _sb(32, B16),
    "lift": _sb(256, B16), "ramp": _sb(512, B16), "liftG": _sb(512, F32),
    "pi": _sb(4, I32), "pa": _sb(4, I32),
    "OBf": _sb(128, F32), "If": _sb(128, F32), "Hf": _sb(128, F32),
    "NOH": _sb(128, B16), "OB": _sb(128, B16), "NOB": _sb(128, B16), "OB40": _sb(128, B16),
    "TriEr": _sb(128, B16), "NTriU": _sb(128, B16),
    "col": _sb(20, F32), "pat": _sb(384, F32),
    "rp5": _sb(130, F32), "r26": _sb(130, B16), "c26": _sb(130, B16), "c25": _sb(256, B16), "ones": _sb(256, B16),
    "nil": _sb(256, B16), "dl": _sb(48, F32), "uc": _sb(4, F32),
    "ea16": _sb(8, U16), "eb16": _sb(8, U16), "af": _sb(8, F32), "bf": _sb(8, F32), "amb": _sb(8, F32),
    "em": _sb(800, B16), "cl": _sb(V, B16), "gt": _sb(800, B16), "ripe": _sb(800, B16), "cum": _sb(800, B16),
    "cnt": _sb(8, F32), "cs": _sb(2, F32), "vs16": _sb(2, U16),
    "xa": _sb(32, F32), "dd": _sb(32, F32), "ez": _sb(32, F32), "ef": _sb(2, F32), "et": _sb(2, F32), "gv": _sb(2, F32),
    "RL": _sb(34, F32), "vsb": _sb(32, F32), "o16": _sb(26, U16), "R16": _sb(26, U16), "giv16": _sb(26, U16),
    "own": _sb(130, B16), "osc": _sb(130, B16), "oy": _sb(130, F32),
    "off16": _sb(26, U16), "PA": _sb(RQ, F32), "PB": _sb(RQ, F32), "SW": _sb(5 * RQ, F32),
    "Pw0": _sb(256, F32), "Pw1": _sb(256, F32),
    "z": _sb(256, F32), "z2": _sb(256, F32), "r16": _sb(256, U16), "rl16": _sb(16, U16), "rlf": _sb(16, F32),
    "E": ("sbuf", [128, 16, 256], B16), "Ed": _sb(256, B16), "TM": _sb(256, B16), "emr": _sb(256, B16),
    "wg": _sb(256, F32), "erg": _sb(256, F32), "t0": _sb(256, F32), "gm": _sb(256, F32), "mm": _sb(256, F32),
    "acc": _sb(256, F32), "accW": _sb(5 * RQ, F32),
    "k": _sb(256, F32), "od16": _sb(16, U16), "ol16": _sb(16, U16), "of16": _sb(16, U16), "w16": _sb(16, U16),
    "p16": _sb(8, U16), "liftx": _sb(32, F32),
    "lc": _sb(128, F32), "clr": _sb(32, F32),
    "psS": ("psum", [128, 1024], F32), "psD": ("psum", [128, 1024], F32), "psE": ("psum", [128, 1024], F32),
    "psG": ("psum", [128, 512], F32), "psH": ("psum", [128, 512], F32),
}
SEMAPHORES = (["cv", "cs", "ct", "cg", "lx0", "lx1", "lx2", "ld1", "ld2", "ld3", "ld4", "st0", "st1", "sn", "an", "ah1", "ah2"]
              + ["%s%d" % (k, t) for k in ("sp", "sr", "ap", "ar") for t in range(RO)]
              + ["sx%d_%d" % (t, c) for t in range(RO) for c in range(3)]
              + ["ax%d_%d_%d" % (t, c, q) for t in range(RO) for c in range(3) for q in range(N)])


def _hit(a, b):
    return any(x[0] == y[0] and x[1] < y[2] and y[1] < x[2] and (x[3] != y[3] or (x[1] - y[1]) % x[3] == 0)
               for x in a for y in b)


def _needs(ops):
    users = {}
    for i, o in enumerate(ops):
        names = set(x[0] for x in o["r"] + o["w"] + o["after"])
        earlier = sorted(set(j for n in names for j in users.get(n, [])))
        for n in names:
            users.setdefault(n, []).append(i)
        wr = o["w"] + o["after"]
        pp = [x for x in o["r"] + wr if x[0].startswith("ps")]
        o["need"], o["past"] = set(), 0
        for j in reversed(earlier):
            p = ops[j]
            if not o["past"] >> j & 1 and (_hit(o["r"], p["w"]) or _hit(wr, p["w"]) or _hit(wr, p["r"]) or _hit(pp, p["r"])):
                o["need"].add(j)
                o["past"] |= p["past"] | 1 << j


def _order(ops):
    n = len(ops)
    pre, suc = [[] for _ in ops], [[] for _ in ops]
    for i, o in enumerate(ops):
        o["pre"] = sorted(o["need"] | set(o["behind"]))
        for j in o["pre"]:
            gap = 0.0 if ops[j]["e"] == o["e"] == "t" else SYNC + ops[j]["fly"]
            if o["f"] and j not in o["need"]:
                gap = 0.0
            pre[i].append((j, gap))
            suc[j].append((i, gap))
    hold, eng = [o["hold"] for o in ops], [o["e"] for o in ops]
    shape = tuple(hold)
    if shape in PLANS:
        at = dict((i, k) for k, i in enumerate(PLANS[shape]))
        if all(at[j] < at[i] for i in range(n) for j, gap in pre[i]):
            return PLANS[shape]

    def place(key, pre, way):
        key = list(key)
        for i in range(n)[::way]:
            for j, gap in pre[i]:
                if key[j] > key[i]:
                    key[i] = key[j]
        start, begin, finish = [0.0] * n, {}, {}
        for i in sorted(range(n)[::way], key=lambda i: key[i]):
            at, d = 0.0, hold[i]
            for j, gap in pre[i]:
                if start[j] + hold[j] + gap > at:
                    at = start[j] + hold[j] + gap
            if eng[i]:
                b, f = begin.setdefault(eng[i], []), finish.setdefault(eng[i], [])
                k, hi = 0, len(f)
                while k < hi:
                    if f[(k + hi) // 2] > at:
                        hi = (k + hi) // 2
                    else:
                        k = (k + hi) // 2 + 1
                while k < len(b) and b[k] < at + d - 1e-6:
                    at = max(at, f[k])
                    k += 1
                b.insert(k, at)
                f.insert(k, at + d)
            start[i] = at
        return start

    def tighten(start):
        late = place([-start[i] - hold[i] for i in range(n)], suc, -1)
        start = place([-late[i] - hold[i] for i in range(n)], pre, 1)
        return max(start[i] + hold[i] for i in range(n)), start

    seed = [1]

    def chance():
        seed[0] = (seed[0] * 1103515245 + 12345) % 2 ** 31
        return seed[0] / 2.0 ** 31

    best = now = tighten(place(range(n), pre, 1))
    for turn in range(TURNS):
        by, mid, far = 300 + 1200 * chance(), now[0] * chance(), 5000 + 25000 * chance()
        new = tighten(place([s + by * (2 * chance() - 1) if abs(s - mid) < far else s for s in now[1]], pre, 1))
        if new[0] <= now[0] + 100:
            now = new
        if new[0] < best[0]:
            best = new
    PLANS[shape] = sorted(range(n), key=lambda i: (best[1][i], i))
    PLANS["end"] = best[0]
    return PLANS[shape]


def _emit(g, T, ops):
    queue = {"v": g.vector, "s": g.scalar, "t": g.tensor, "g": g, "y": g.sync}
    counter = {"v": "cv", "s": "cs", "t": "ct", "g": "cg"}
    known = {e: {} for e in queue}
    seq = {e: 0 for e in queue}
    _needs(ops)
    order = _order(ops)
    place = dict((i, k) for k, i in enumerate(order))
    for i in order:
        o = ops[i]
        e = o["e"]
        o["waits"] = []
        o["sig"] = False
        if o["f"] is None:
            o["key"], o["val"], o["clock"] = ("a", i), 1, {}
            continue
        for p in [ops[j] for j in sorted(o["need"], key=lambda j: -place[j])]:
            if p["e"] == e and p["sem"] is None and o["sem"] is None:
                if e == "t" or not (_hit(o["r"], p["w"]) or _hit(o["w"], p["w"] + p["r"])):
                    continue
            if known[e].get(p["key"], 0) >= p["val"]:
                continue
            o["waits"].append(p)
            p["sig"] = True
            for k, v in list(p["clock"].items()) + [(p["key"], p["val"])]:
                if known[e].get(k, 0) < v:
                    known[e][k] = v
        o["clock"] = dict(known[e])
        if o["sem"] is None:
            seq[e] += 1
            o["key"], o["val"] = e, seq[e]
        else:
            o["key"], o["val"] = ("a", i), 1
    ops = [ops[i] for i in order]
    total = {e: 0 for e in counter}
    for o in ops:
        if o["sem"] is None and o["sig"]:
            total[o["e"]] += 1
            o["sv"] = (counter[o["e"]], total[o["e"]])
        elif o["sem"] is not None:
            o["sv"] = o["sem"]
    seen = {}
    for o in ops:
        if o["f"] is None:
            continue
        for p in o["waits"]:
            queue[o["e"]].wait_ge(T.sem[p["sv"][0]], p["sv"][1])
            seen[p["sv"][0]] = max(seen.get(p["sv"][0], 0), p["sv"][1])
        ins = o["f"](queue[o["e"]])
        if o["sem"] is None and o["sig"]:
            ins.then_inc(T.sem[counter[o["e"]]], 1)
    for o in ops:
        if o["sem"] is not None and seen.get(o["sem"][0], 0) < o["sem"][1]:
            g.wait_ge(T.sem[o["sem"][0]], o["sem"][1])


def _helper(q, T, topo):
    far = [c for c in T.cores if c not in topo.cores_of(T.cores[q])]
    return [c for c in topo.cores_of(far[0]) if c not in T.cores and topo.die(c) == topo.die(T.cores[q])][0]


def _hand_on(g, core, q, T, topo):
    here = [c for c in T.cores if c in topo.cores_of(core)]
    for t in range(1, RO):
        for c, (a, b) in enumerate(PIECES):
            if WIDE[c]:
                part = T["tab%d" % (t % 2)][:, q * V + a:q * V + b]
                g.wait_ge(T.sem["ah%d" % t], len(topo.engines(T.cores[q], core)))
                trs = []
                for k, dst in enumerate(here):
                    rid, pid = topo.addr(dst, core)
                    es = topo.engines(core, dst)
                    es = es[len(es) // 2 * k:len(es) // 2 * (k + 1)]
                    trs.append(RemoteDMATransfer(dst_ids=[DstId(rid=rid, pnc=pid)], dma_engine_mask=sum(1 << e for e in es),
                                                 remote_sem=T.sem["ax%d_%d_%d" % (t, c, q)], src=part, dst=part))
                g.remote_dma_fused(trs, local_sem=T.sem["sx%d_%d" % (t, c)])
                g.wait_ge(T.sem["sx%d_%d" % (t, c)], 2 * len(es))


def rank_program(g, core, T, topo):
    me = T.rank_of(core)
    if me is None:
        for q in range(N):
            if core == _helper(q, T, topo):
                _hand_on(g, core, q, T, topo)
        return
    ops = []
    sends, moves = [], []

    def A(name, lo=0, hi=None, step=1):
        hi = SCRATCH[name][1][1] if hi is None else hi
        ap = T[name][:, lo:hi] if step == 1 else T[name][:, lo:hi:step]
        n = (hi - lo + step - 1) // step
        if name.startswith("ps"):
            lo, hi, step = lo // 512 * 512, (hi + 511) // 512 * 512, 1
        return (ap, [(name, lo, hi, step)], [], n, 2 if SCRATCH[name][2] in (B16, U16) else 4, name.startswith("ps"))

    def A3(name, lo, hi, a, b):
        ap = T[name][:, lo, a:b] if hi == lo + 1 else T[name][:, lo:hi, a:b]
        return (ap, [(name, lo, hi, 1)], [], (hi - lo) * (b - a), 2, False)

    def X(win, off):
        return (win[0].indirect(off[0]), win[1], off[1], 16 * off[3], 4, False)

    def add(e, f, hold, fly, outs, ins, sem=None, after=(), behind=()):
        r, w = [], []
        for a in ins:
            if isinstance(a, tuple):
                r += a[1] + a[2]
        for a in outs:
            w += a[1]
            r += a[2]
        ops.append({"e": e, "f": f, "hold": hold, "fly": fly, "r": r, "w": w, "sem": sem,
                    "after": [x for a in after for x in a[1]], "behind": list(behind)})

    def P(a):
        return a[0] if isinstance(a, tuple) else a

    def vtime(o, ins, k=1.0):
        if o[2]:
            return 50 + SC * CY * o[3]
        if ins and ins[0][2]:
            return 50 + GA * CY * o[3]
        return VC + CY * k * o[3] * (0.5 if all(a[4] == 2 for a in [o] + ins) else 1)

    def cp(o, a):
        add("v", lambda q: q.tensor_copy(o[0], a[0]), vtime(o, [a]), 0, [o], [a])

    def ms(o, c):
        add("v", lambda q: q.memset(o[0], c), vtime(o, []), 0, [o], [])

    def tt(o, a, b, op):
        add("v", lambda q: q.tensor_tensor(o[0], a[0], b[0], op), vtime(o, [a, b], 1 if a[5] or b[5] else 2), 0, [o], [a, b])

    def ts(o, a, s1, op0, s2=None, op1=None):
        if s2 is None:
            add("v", lambda q: q.tensor_scalar(o[0], a[0], P(s1), None, op0), vtime(o, [a]), 0, [o], [a, s1])
        else:
            add("v", lambda q: q.tensor_scalar(o[0], a[0], P(s1), P(s2), op0, op1), vtime(o, [a]), 0, [o], [a, s1, s2])

    def scan(o, a, b, init, op0, op1):
        add("v", lambda q: q.tensor_tensor_scan(o[0], a[0], b[0], P(init), op0, op1), vtime(o, [a, b]), 0, [o], [a, b, init])

    def act(o, a, fn, bias=None, scale=None, acc=None):
        kw = {}
        if bias is not None:
            kw["bias"] = P(bias)
        if scale is not None:
            kw["scale"] = P(scale)
        if acc is not None:
            kw["accum_out"] = acc[0]
        add("s", lambda q: q.activation(o[0], a[0], fn, **kw), 65 + CY * a[3] * GA if a[2] else SCALL + CY * a[3], 0,
            [o] + ([acc] if acc else []), [a, bias, scale])

    def mm(o, l, r, start, stop):
        add("t", lambda q: q.matmul(o[0], l[0], r[0], start, stop), PE * max(64, r[3]) * (4 if r[4] == 4 else 1), 0, [o], [l, r])

    def iota(o, pattern, base, cm, whole=False):
        kw = {} if whole else {"allow_small_or_imprecise_dtypes": True}
        add("g", lambda q: q.iota(o[0], pattern, base, cm, **kw), 130 + 2 * CY * o[3], 0, [o], [], behind=sends[-1:])

    def zero(o):
        iota(o, [[0, o[3]]], 0, 0)

    def dma(e, o, a, sem):
        add(e, lambda q: q.dma_start(o[0], a[0]).then_inc(T.sem[sem], 16), 50, 2200, [o], [a], sem=(sem, 16))

    def hbm(name, a=None, b=None):
        return (T[name][:] if a is None else T[name][:, a:b], [(name, 0, 1, 1)], [])

    others = [q for q in range(N) if q != me]
    near = [q for q in others if T.cores[q] in topo.cores_of(core)]
    far = [q for q in others if q not in near]
    efar = topo.engines(core, T.cores[far[0]])
    enear = [e for e in topo.engines(core, T.cores[near[0]]) if e not in efar]

    def bits(es):
        return sum(1 << e for e in es)

    def XIN(t, owner, src, a, b):
        o = (3 * (t % 2) + (src - owner - 1) % N) * V
        return A("xin", o + a, o + b)

    def send(items, sem, after=(), lane="d"):
        trs = []
        for q, src, dst, es, rs in items:
            rid, pid = topo.addr(T.cores[q] if q >= 0 else _helper(me, T, topo), core)
            trs.append(RemoteDMATransfer(dst_ids=[DstId(rid=rid, pnc=pid)], dma_engine_mask=bits(es),
                                         remote_sem=T.sem[rs], src=src[0], dst=dst))
        add("g", lambda q: q.remote_dma_fused(trs, local_sem=T.sem[sem]), 150, HOP + (0 if sends else FIRST),
            [], [it[1] for it in items], sem=(sem, sum(len(it[3]) for it in items)), after=after, behind=sends[-1:])
        sends.append(len(ops) - 1)
        row = items[0][1][3] * items[0][1][4]
        if lane == "n":
            add(lane, None, 64 / h * (ROW + row / RATE) + FIRST / 2, 0, [], [], behind=sends[-1:])
        elif lane == "r":
            add("d", None, max(64 / h * (ROW + row / RATE), 128 * row / PORT), 0, [], [], behind=sends[-1:] + moves[-1:])
        else:
            add(lane, None, max(128 / h * (ROW + row / RATE), 256 * row / PORT), 0, [], [], behind=sends[-1:] + moves[-1:])
        moves.append(len(ops) - 1)

    def arrive(outs, sem, n):
        add(None, None, 0, 200, outs, [], sem=(sem, n), behind=moves[-1:])

    h = len(efar) // 2
    eng = {far[0]: efar[:h], far[1]: efar[h:], near[0]: enear}

    def TAB(t, a=0, b=3080):
        return A("tab%d" % (t % 2), a, b)

    def x(t, a, b):
        return TAB(t, me * V + a, me * V + b)

    def send_narrow(a, b, c):
        send([(q, A("xu", a, b), XIN(0, q, me, a, b)[0], eng[q], "ax0_%d_%d" % (c, me)) for q in far], "sx0_%d" % c)
        for q in far:
            arrive([XIN(0, me, q, a, b)], "ax0_%d_%d" % (c, q), len(eng[q]))

    def send_new(t, a, b, c):
        if WIDE[c]:
            send([(near[0], x(t, a, b), x(t, a, b)[0], enear, "ax%d_%d_%d" % (t, c, me)),
                  (-1, x(t, a, b), x(t, a, b)[0], efar, "ah%d" % t)], "sx%d_%d" % (t, c), lane="r")
            arrive([TAB(t, near[0] * V + a, near[0] * V + b)], "ax%d_%d_%d" % (t, c, near[0]), len(enear))
            for q in far:
                arrive([TAB(t, q * V + a, q * V + b)], "ax%d_%d_%d" % (t, c, q), 8)
                ops[-1]["hold"] = HOP + 16 * (ROW + 4 * (b - a) / RATE) + 500 + (FIRST if t == 1 else 0)
            return
        q, m, sem = near[0], (a + b) // 2, "ax%d_%d_%d" % (t, c, me)
        send([(q, A("xu", a, b), XIN(t, q, me, a, b)[0], eng[q], sem) for q in far]
             + [(q, x(t, a, m), x(t, a, m)[0], enear[:h], sem), (q, x(t, m, b), x(t, m, b)[0], enear[h:], sem)], "sx%d_%d" % (t, c))
        arrive([TAB(t, q * V + a, q * V + b)], "ax%d_%d_%d" % (t, c, q), len(enear))
        for q in far:
            arrive([XIN(t, me, q, a, b)], "ax%d_%d_%d" % (t, c, q), len(eng[q]))
        widen(t, far, a, b)

    def widen(t, ranks, a, b):
        for q in ranks:
            cp(TAB(t, q * V + a, q * V + b), XIN(t, me, q, a, b))

    def F(t, a=0, b=DQ + 256, step=1):
        return A("F", 4 * EARLY * (1 - t) + a, 4 * EARLY * (1 - t) + b, step)

    rcol, rm1, fix, nfix, b0, b1, fx2, r0, cls, clb, r1, c4, cw, pm, pa, px, py = [A("col", j, j + 1) for j in range(17)]
    dl, dl2, dlq = A("dl", 0, 16), A("dl", 16, 32), A("dl", 32, 48)
    ka, kb, kc, kd, ke, kf, kg = [A("k", 16 * j, 16 * j + 16) for j in range(7)]
    kh, ki, kj, kk, kl = [A("k", 16 * j, 16 * j + 16) for j in range(11, 16)]
    pat = A("pat", 0, 256)

    I1, I2 = A("z2", 0, 128), A("z2", 128, 256)
    for c, (a, b) in enumerate(OPENING):
        dma("y", A("xi", a, b), hbm("x0", a, b), "lx%d" % c)
    dma("y", A("li"), hbm("l0"), "ld1")
    dma("y", A("eai", 0, 6), hbm("ea"), "ld2")
    dma("y", A("ebi", 0, 6), hbm("eb"), "ld3")
    dma("y", A("ui", 0, 3), hbm("u"), "ld4")
    iota(I2, [[16, 8], [0, 16]], 0, -1)
    iota(I1, [[1, 128]], 0, -1)
    iota(A("pi", 0, 1), [[0, 1]], 0, 1, True)
    iota(A("mm"), [[0, 16], [1, 16]], 0, 0)
    iota(kd, [[16, 16]], 0, 0)
    for c, (a, b) in enumerate(OPENING):
        cp(A("xu", a, b), A("xi", a, b))
        send_narrow(a, b, c)
    cp(x(0, 0, V), A("xi"))
    send([(near[0], x(0, 0, V), x(0, 0, V)[0], enear, "an")], "sn", lane="n")
    arrive([TAB(0, near[0] * V, near[0] * V + V)], "an", len(enear))
    for t in range(2):
        ms(TAB(t, NONE, 3080), 0.0)

    def fill(o, c):
        act(o, A("mm", 0, o[3]), AF.Identity, bias=c, scale=0.0)

    ms(A("out0"), 0.0)
    act(A("out1"), A("out0"), AF.Copy)
    fill(A("nil"), 0.0)
    fill(A("ones"), 1.0)
    fill(A("c25"), 2.5 / 16)
    act(A("Lf", SP, PL), A("out0", 0, PL - SP), AF.Copy)
    fill(A("rp5"), 0.0)
    fill(A("Mx", 384, 512), 0.0)
    fill(A("kill", 0, 24), -float(2 ** 20))
    fill(A("kill", 24, 32), 0.0)
    fill(A("ripe", V, 800), 2.0)
    ts(A("PA", 0, 128), I2, -15.0, OP.max, 0.0, OP.min)
    fill(A("Lf", V, SP), float(NONE))
    tt(A("OBf"), A("PA", 0, 128), I2, OP.is_equal)
    ts(A("If"), I1, 0.0, OP.is_equal)
    ts(A("pa", 0, 1), A("pi", 0, 1), 15, OP.bitwise_and)
    ts(A("PA", 128, 256), I1, 0.0, OP.is_gt)
    ts(A("PA", 256, 384), I1, 0.0, OP.is_lt, -1.0, OP.mult)
    cp(rcol, A("pa", 0, 1))
    act(A("OB"), A("OBf"), AF.Copy)
    act(A("PB", 128, 256), A("If"), AF.Copy, scale=-128.0)
    act(A("z", 0, 128), A("If"), AF.Copy, scale=-4096.0)
    act(A("Hf"), A("If"), AF.Copy, scale=0.5)
    act(A("NOH"), A("OBf"), AF.Copy, scale=-0.5)
    act(A("NOB"), A("OBf"), AF.Copy, scale=-1.0)
    tt(A("PB", 0, 128), A("PA", 128, 256), A("OBf"), OP.mult)
    tt(A("PB", 256, 384), A("PA", 256, 384), A("OBf"), OP.mult)
    iota(A("lift"), [[0, 8], [4096, 32]], 0, 0)
    iota(A("G", 0, 512), [[4096, 32], [0, 16]], 0, 0)
    act(A("liftG"), A("G", 0, 512), AF.Copy, scale=16.0)
    iota(A("T3", 0, V), [[0, 3], [4096, 256]], 0, 0)
    fill(A("T3", V, WN), 0.0)
    iota(A("T1"), [[1, 3104]], 0, 0)
    zero(A("accW"))
    zero(A("D0", 0, DUM))
    for k in range(0, FOLD, 256):
        act(A("RP", k, k + 256), A("mm"), AF.Sign)
    fill(A("ramp", 1, 512, 2), 0.0)
    act(A("ramp", 0, 512, 2), A("T3", 0, 256), AF.Copy)
    tt(A("TriEr"), A("PB", 0, 128), A("PB", 128, 256), OP.add)
    tt(A("NTriU"), A("PB", 256, 384), A("z", 0, 128), OP.add)
    ts(r0, rcol, 0.0, OP.is_equal)
    ts(b0, rcol, -2.0, OP.mult, -1.0, OP.add)
    ts(b1, rcol, -2.0, OP.mult, -33.0, OP.add)
    ts(A("TM"), A("mm"), rcol, OP.is_gt)
    ts(rm1, r0, 16.0, OP.mult, rcol, OP.add)
    ts(fix, r0, -2 * BIG, OP.mult, BIG, OP.add)
    ts(A("t0", 0, 128), A("mm", 0, 128), rcol, OP.is_equal, -BIG, OP.mult)
    ts(dl2, kd, rcol, OP.add, float(WN), OP.add)
    ts(rm1, rm1, -1.0, OP.add)
    ts(nfix, fix, -1.0, OP.mult)
    ts(fx2, fix, 1.0 / 4096, OP.mult, -0.375, OP.add)
    ts(dl, dl2, float(DUM - WN), OP.add)
    ts(dlq, dl2, float(DQ - WN), OP.add)
    ts(A("t0", 128, 256), A("mm", 0, 128), rm1, OP.is_equal, 2 * BIG, OP.mult)
    ts(cls, r0, -2.0, OP.mult, 1.0, OP.add)
    ts(clb, r0, 19.0, OP.mult, -15.0, OP.add)
    ts(r1, rcol, 1.0, OP.is_equal, -40.0, OP.mult)
    ts(c4, nfix, 2.5, OP.add)
    ts(cw, nfix, float(NONE), OP.add)
    ts(pm, rcol, 8.0, OP.is_lt, 4.0, OP.mult)
    ts(pa, rcol, float(DQ), OP.add)
    ts(px, rcol, 8.0, OP.is_ge)
    ts(r1, r0, 40.0, OP.mult, r1, OP.add)
    ts(pa, pa, px, OP.mult)
    tt(A("pat", 0, 128), A("t0", 0, 128), A("t0", 128, 256), OP.add)
    act(A("OB40"), A("OBf"), AF.Copy, scale=r1)
    for n in (128, 256):
        act(A("pat", n, n + 128), A("pat", 0, 128), AF.Copy)
    cp(A("Lf", 0, V), A("li"))
    fill(A("r26"), 1.0)
    iota(A("c26"), [[0, 26], [RQ // 16, 5]], 256, 0)
    fill(A("rp5", 0, 130, 5), 16384.0)
    fill(A("r26", 0, 130, 26), 0.0)
    fill(A("clr", 24, 32), 0.0)
    ts(A("af", 0, 6), A("eai", 0, 6), float(me * V), OP.add)
    cp(A("bf", 0, 6), A("ebi", 0, 6))
    cp(A("eb16", 0, 6), A("ebi", 0, 6))
    ts(A("uc", 0, 3), A("ui", 0, 3), -0.25, OP.add)
    cp(A("ea16", 0, 6), A("af", 0, 6))
    tt(A("amb", 0, 6), A("af", 0, 6), A("bf", 0, 6), OP.subtract)
    for a, b in OPENING:
        widen(0, far, a, b)

    ring = [0]

    def stage(a, lo=0, hi=None, step=1):
        return A(("psH", "psG", "psH")[a // 256], lo, 2 * min(256, EARLY - a) if hi is None else hi, step)

    def half(a, b):
        return A("psS", a + 256, b + 256) if a < 512 else A("psD", a + 512 - LAST, b + 512 - LAST)

    def half_open(t, a, b, up):
        mm(half(a, b), A("Hf"), x(t, a, b), True, False)
        if up:
            mm(half(a, a + up[3]), A("NOH"), up, False, False)

    def gather(t, a, b):
        joins = t and a < EARLY
        if joins:
            mm(stage(a), A("OB"), A("ramp", 0, 2 * (b - a)), True, False)
            mm(stage(a, 0, 2 * (b - a), 2), A("OB"), A("out%d" % (t - 1), a, b), False, False)
            if a == 512:
                second(t, a, b)
        mine = OWN if a == t == 0 else 0
        if not joins:
            half_open(t, a, b, A("lift", 0, mine) if mine else None)
        n = 64 if a < LAST else 32
        for v in range(a, b, n):
            go, mo = 1024 * (ring[0] % GS), 1024 * (ring[0] % 4)
            ring[0] += 1
            if v < a + mine:
                for k in (0, 512):
                    tt(A("G", go + k, go + k + 512), X(TAB(t), A("L16", v + k // 16, v + k // 16 + 32)), A("liftG"), OP.add)
                    scan(A("MS", mo + k + 1, mo + k + 512, 2), A("G", go + k, go + k + 512, 2), A("G", go + k + 1, go + k + 512, 2),
                         0.0, OP.max, OP.max)
            else:
                act(A("G", go, go + 16 * n), X(TAB(t), A("L16", v, v + n)), AF.Copy)
                w = min(FOLD, 16 * n)
                for k in range(0, 16 * n, w):
                    scan(A("MS", mo + k, mo + k + w), A("RP", 0, w), A("G", go + k, go + k + w), 0.0, OP.mult, OP.max)
            Mv = A("MS", mo + 15, mo + 16 * n, 16)
            if joins:
                mm(stage(a, 2 * (v - a), 2 * (v - a + n), 2), A("If"), Mv, False, v + n == LAST)
            else:
                mm(half(v, v + n), A("Hf"), Mv, False, v + n == b)

    def second(t, a, b):
        mm(stage(a, 1, 2 * (b - a), 2), A("If"), F(t - 1, 4 * a + 1, 4 * b, 4), False, a < 512)

    def join(t, a, b):
        scan(A("Q", 2 * a, 2 * b), stage(a), F(t - 1, 4 * a, 4 * b, 2), 0.0, OP.max, OP.max)
        half_open(t, a, b, A("ramp", 0, 2 * (b - a), 2))
        mm(half(a, b), A("Hf"), A("Q", 2 * a + 1, 2 * b, 2), False, True)

    def degrees():
        act(A("em", 0, V), A("Lf", 0, V), AF.Relu, bias=1.0 - NONE)
        for a, b in ((0, 512), (512, V)):
            mm(A("psE", a, b), A("OB"), A("em", a, b), True, True)
        act(A("cl"), A("psE", 0, V), AF.Relu, bias=clb, scale=cls)

    def choose(t, k):
        a, b = BLOCKS[k]
        mm(A("psE", a, b), A("OB40"), A("cl", a, b), True, False)
        tt(A("gt", a, b), half(a, b), x(t, a, b), OP.is_lt)
        mm(A("psE", a, b), A("OB"), A("gt", a, b), False, True)
        bar = 11.5
        if RIPE[t][k] == "s":
            act(A("ripe", a, b), A("psE", a, b), AF.Sign, bias=-bar)
        else:
            ts(A("ripe", a, b), A("psE", a, b), bar, OP.is_gt, 2.0, OP.mult)
        e = 800 if b == V else b
        scan(A("cum", a, e), A("ones" if RIPE[t][k] == "s" else "nil", 0, e - a), A("ripe", a, e),
             A("cum", a - 1, a) if a else 0.0, OP.add, OP.add)

    def places(k, a, b):
        act(A("em", a, b), A("cum", a, b), AF.Sign, bias=b0, acc=A("cnt", 2 * k, 2 * k + 1))
        act(A("gt", a, b), A("cum", a, b), AF.Sign, bias=b1, acc=A("cnt", 2 * k + 1, 2 * k + 2))

    def new_x(t, c):
        a, b = PIECES[c]
        ts(A("xu", a, b), half(a, b), A("uc", t, t + 1), OP.add)
        if t == RO - 1:
            cp(A("Q", a, b), A("xu", a, b))
        else:
            cp(x(t + 1, a, b), A("xu", a, b))
            send_new(t + 1, a, b, c)

    def edges(t):
        e2 = (2 * t, 2 * t + 2)
        act(A("xa"), X(TAB(t), A("ea16", *e2)), AF.Copy)
        tt(A("dd"), X(TAB(t), A("eb16", *e2)), A("xa"), OP.subtract)
        mm(A("psG", 160, 192), A("OBf"), A("dd"), True, True)
        scan(A("ez"), A("psG", 160, 192), A("pat", 0, 32), nfix, OP.min, OP.add)
        ts(A("ef"), A("ez", 15, 32, 16), fix, OP.add, 0.0, OP.is_ge)
        tt(A("et"), A("ef"), A("amb", *e2), OP.mult)
        tt(A("RL", 0, 2), A("et"), A("bf", *e2), OP.add)
        tt(A("gv"), A("af", *e2), A("et"), OP.subtract)
        cp(A("giv16", 0, 2), A("gv"))

    def free_slots():
        for d in range(4):
            iota(A("SW", RQ * d, RQ * d + 64), [[0, 64]], 4096 * SP, 0)

    def values(t):
        for k, (a, b) in enumerate(BLOCKS):
            if t == 0 or a >= 512:
                gather(t, a, b)
            if t and a < EARLY:
                join(t, a, b)
            choose(t, k)
            for c, piece in enumerate(PIECES):
                if b == piece[1]:
                    new_x(t, c)
            if k:
                places(k - 1, 0 if k == 1 else a, 800 if b == V else b)
        tt(A("cs"), A("cnt", 0, 2), A("cnt", 2, 4), OP.add)
        ts(A("cs"), A("cs"), -0.5, OP.mult, 400.0, OP.add)
        for c in range(2):
            ts(A("vs16", c, c + 1), A("cnt", 4 + c, 5 + c), -0.5, OP.mult, A("cs", c, c + 1), OP.add)

    def requests(t):
        mm(A("psG", 0, 130), A("OB"), A("c26"), True, False)
        cp(A("RL", 2, 34), X(A("Lf", 0, 800), A("vs16")))
        cp(A("vsb"), X(A("T1", me * V, me * V + 800), A("vs16")))
        ts(A("o16"), A("RL", 0, 26), 1.0 / V, OP.mult, -0.4995, OP.add)
        cp(A("giv16", 2, 26), A("vsb", 0, 24))
        act(A("PB"), X(A("T1"), A("giv16")), AF.Identity, bias=float(NONE), scale=-1.0)
        ts(A("k", 112, 138), A("o16"), -float(V), OP.mult)
        tt(A("k", 144, 170), A("k", 112, 138), A("RL", 0, 26), OP.add)
        cp(A("R16"), A("k", 144, 170))
        act(A("PA"), X(A("T1", 0, V), A("R16")), AF.Copy, scale=4096.0)
        for d in range(5):
            ts(A("own", 26 * d, 26 * d + 26), A("o16"), float(d), OP.is_equal)
            mm(A("psG", d, 130, 5), A("NTriU"), A("own", 26 * d, 26 * d + 26), False, False)
        scan(A("osc"), A("r26"), A("own"), 0.0, OP.mult, OP.add)
        for d in range(5):
            mm(A("psG", d, 130, 5), A("OB"), A("osc", 26 * d, 26 * d + 26), False, d == 4)
        scan(A("oy"), A("rp5"), A("psG", 0, 130), 0.0, OP.add, OP.min)
        ts(A("off16"), A("oy", 4, 130, 5), -1.0, OP.add)
        tt(X(A("SW"), A("off16")), A("PA"), A("PB"), OP.add)
        Pw = "Pw%d" % (t % 2)
        send([(q, A("SW", RQ * q, RQ * q + 64), A(Pw, 64 * me, 64 * me + 64)[0], eng[q], "ap%d" % t) for q in others],
             "sp%d" % t, after=[A("accW")])
        arrive([A(Pw, 64 * q, 64 * q + 64) for q in others], "ap%d" % t, 2 * h + len(enear))
        act(A(Pw, 64 * me, 64 * me + 64), A("SW", RQ * me, RQ * me + 64), AF.Copy)

    def verdicts(t):
        Pw = A("Pw%d" % (t % 2))
        mm(A("psH", 0, 256), A("OB"), A("c25"), True, False)
        scan(A("z"), Pw, pat, nfix, OP.min, OP.add)
        ts(A("r16"), Pw, 1.0 / 4096, OP.mult, -0.375, OP.add)
        ts(A("rl16"), A("z", 15, 256, 16), 1.0 / 4096, OP.mult, fx2, OP.add)
        act(A("emr"), X(A("Lf", 0, WN), A("rl16")), AF.Relu, bias=1.0 - NONE)
        cp(A("rlf"), A("rl16"))
        mm(A("psE", 0, 256), A("OB"), A("emr"), True, True)
        mm(A("psD", 0, 256), A("TriEr"), A("emr"), True, True)
        act(A("wg"), A("psE", 0, 256), AF.Relu, bias=2.5, scale=-1.0)
        act(A("erg"), A("psD", 0, 256), AF.Relu, bias=-125.5, scale=-1.0)
        for c in range(16):
            ts(A3("E", c, c + 1, 0, 256 - 16 * c), A("r16", 16 * c, 256), A("rlf", c, c + 1), OP.is_equal)
            if c < 15:
                mm(A("psH", 16 * c + 16, 256), A("NOB"), A3("E", c, c + 1, 16, 256 - 16 * c), False, False)
        tt(A("Ed"), A3("E", 0, 16, 0, 16), A("TM"), OP.mult)
        mm(A("psH", 0, 256), A("NOB"), A("Ed"), False, True)
        tt(A("acc"), A("psH", 0, 256), A("wg"), OP.is_gt)
        send([(q, A("acc", 64 * q, 64 * q + 64), A("accW", RQ * me, RQ * me + 64)[0], eng[q], "ar%d" % t) for q in others], "sr%d" % t,
             after=[A("xin", 3 * V * (t % 2), 3 * V * (t % 2 + 1))])
        arrive([A("accW", RQ * q, RQ * q + 64) for q in others], "ar%d" % t, 2 * h + len(enear))
        act(A("accW", RQ * me, RQ * me + 64), A("acc", 64 * me, 64 * me + 64), AF.Copy)
        act(ke, A("rlf"), AF.Identity, bias=cw, scale=4096.0)
        tt(kf, ke, A("z", 15, 256, 16), OP.subtract)
        cp(A("w16"), kf)
        act(A("gm"), X(A("T1"), A("w16")), AF.Identity, bias=-float(NONE))
        scan(A("z2"), A("psH", 0, 256), pat, nfix, OP.min, OP.add)
        tt(A("mm"), A("psH", 0, 256), A("erg"), OP.is_equal)

    def answers():
        act(A("PA", 0, 384), X(A("accW"), A("off16", 2, 26)), AF.Copy)
        scan(A("PB", 0, 384), A("PA", 0, 384), A("pat"), nfix, OP.min, OP.add)
        ts(A("clr", 0, 24), A("PB", 15, 384, 16), fix, OP.add, float(NONE), OP.mult)

    def lists(t):
        D = "D%d" % (t % 2)
        act(A("wg"), X(A("Lf", 0, WN), A("rl16")), AF.Copy)
        act(kg, A("rlf"), AF.Identity, bias=2.5 * PL)
        ts(ka, A("z2", 15, 256, 16), fix, OP.add, -float(PL), OP.mult)
        tt(kb, ka, kg, OP.add)
        tt(kc, kb, dl, OP.min)
        tt(kd, kb, dl2, OP.min)
        cp(A("od16"), kc)
        cp(A("ol16"), kd)
        tt(X(A(D), A("od16")), A("mm"), A("gm"), OP.mult)
        act(A("erg"), X(A(D, 2 * PL, 2 * PL + WN), A("rl16")), AF.Copy)
        tt(A("gm"), X(A(D, 0, WN), A("rl16")), A("wg"), OP.add)
        tt(A("mm"), X(A(D, PL, PL + WN), A("rl16")), A("gm"), OP.add)
        tt(X(A("Lf"), A("ol16")), A("mm"), A("erg"), OP.add)
        answers()
        cp(A("lc", 0, 32), X(A("Lf", 0, 800), A("vs16")))
        if t == RO - 1:
            tt(X(A("Lf", 0, 800), A("vs16")), A("lc", 0, 32), A("clr"), OP.max)
            return
        tt(A("lc", 32, 64), A("lc", 0, 32), A("clr"), OP.max)
        cp(A("Lx16"), A("lc", 32, 64))
        cp(X(A("Lf", 0, 800), A("vs16")), A("lc", 32, 64))
        cp(A("L16", EARLY, V), A("Lf", EARLY, V))

    def newcomers(t):
        zk = A("z2", 15, 256, 16)
        act(kh, A("rlf"), AF.Identity, bias=c4, scale=4.0)
        ts(ki, zk, nfix, OP.is_lt, 8000.0, OP.mult)
        tt(kj, kh, zk, OP.subtract)
        tt(kk, kj, ki, OP.add)
        tt(kl, kk, dlq, OP.min)
        cp(A("of16"), kl)
        act(A("t0"), X(A("T3"), A("rl16")), AF.Copy, scale=16.0)
        tt(A("z"), X(TAB(t + 1), A("w16")), A("t0"), OP.add)
        tt(X(F(t), A("of16")), A("z"), A("acc"), OP.mult)
        second(t + 1, 0, 256)
        second(t + 1, 256, 512)
        ts(A("p16", 0, 1), A("vs16", 0, 1), 4.0, OP.mult)
        ts(A("p16", 1, 2), A("vs16", 1, 2), pm, OP.mult, pa, OP.add)
        act(A("liftx"), X(A("T3"), A("vs16")), AF.Copy, scale=16.0)
        act(A("PA", 0, 384), X(TAB(t + 1), A("Lx16", 0, 24)), AF.Copy)
        scan(A("Mx", 0, 384), A("RP", 0, 384), A("PA", 0, 384), 0.0, OP.mult, OP.max)
        tt(X(F(t), A("p16", 0, 2)), A("Mx", 15, 512, 16), A("liftx"), OP.add)

    cp(A("L16"), A("li"))
    degrees()
    edges(0)
    for t in range(RO):
        if t:
            verdicts(t - 1)
            cp(X(A("out%d" % (t - 1)), A("vs16")), A("kill"))
            gather(t, 0, 256)
            gather(t, 256, 512)
            free_slots()
            zero(A("D%d" % (t % 2), 0, DUM))
            if t == 1:
                zero(F(1, 0, 4 * EARLY))
            lists(t - 1)
            newcomers(t - 1)
            degrees()
        else:
            free_slots()
        values(t)
        if t == 1:
            cp(A("L16", 0, EARLY), A("Lf", 0, EARLY))
        requests(t)
        if t == 0:
            zero(F(0, 0, 4 * EARLY))
        if t < RO - 1:
            edges(t + 1)

    dma("y", hbm("yx"), A("Q", 0, V), "st0")
    verdicts(RO - 1)
    lists(RO - 1)
    dma("y", hbm("yl"), A("Lf", 0, V), "st1")
    _emit(g, T, ops)
